import numpy as np
import ml_dtypes


def mxq(x, axis, fmt="e4m3"):
    dtype, down = {"e4m3": (ml_dtypes.float8_e4m3fn, 7), "e5m2": (ml_dtypes.float8_e5m2, 14)}[fmt]
    v = np.moveaxis(np.asarray(x, np.float32).astype(ml_dtypes.bfloat16).astype(np.float64), axis, -1)
    blocks = v.reshape(v.shape[:-1] + (-1, 32))
    amax = np.abs(blocks).max(-1, keepdims=True)
    byte = np.maximum(np.where(amax > 0, np.frexp(amax)[1] - 1 + 127, 0) - down, 1)
    scale = np.exp2(byte - 127.0)
    codes = (blocks / scale).astype(np.float32).astype(dtype).astype(np.float64)
    return np.moveaxis((codes * scale).reshape(v.shape), -1, axis)


WIDE = False


def mx_kscale(k):
    if not WIDE:
        return np.ones(k)
    levels = np.array([10, -10, 5, -5, 0])
    if k % 512:
        return np.exp2(np.random.permutation(np.resize(levels, k // 32))).repeat(32)
    a = np.empty((k // 512, 16))
    for p in range(k // 512):
        a[p, :8] = np.random.permutation(np.resize(levels, 8))
        for g in range(8):
            far = levels[np.abs(levels - a[p, g]) >= 10]
            a[p, g + 8] = far[np.random.randint(len(far))]
    return np.exp2(a.ravel()).repeat(32)


def f64(x):
    return np.asarray(x).astype(np.float64)


def striped(idx):
    return np.tile(idx.reshape(-1, 16).T, (8, 1)).astype(np.uint16)


def unstriped(offs):
    return offs[:16].T.reshape(-1).astype(np.int64)


E2M1 = np.array([0.0, 0.5, 1.0, 1.5, 2.0, 3.0, 4.0, 6.0, -0.0, -0.5, -1.0, -1.5, -2.0, -3.0, -4.0, -6.0])


def pack_weight(w, fmt):
    k, n = w.shape
    w = f64(np.asarray(w, np.float32).astype(ml_dtypes.bfloat16)).reshape(k // 32, 32, n)
    amax = np.abs(w).max(1)
    if fmt == "e4m3":
        byte = np.frexp(amax)[1] - 1 + 127 - 7
    else:
        mant, ex = np.frexp(amax / 6.0)
        byte = np.where(mant > 0.5, ex, ex - 1) + 127
    byte = np.clip(np.where(amax > 0, byte, 1), 1, 254)
    scaled = (w * np.exp2(127.0 - byte)[:, None, :]).reshape(k, n).astype(np.float32)
    by_word = np.ascontiguousarray(scaled.reshape(k // 512, 128, 4, n).transpose(0, 1, 3, 2))
    if fmt == "e4m3":
        words = by_word.astype(ml_dtypes.float8_e4m3fn).view(np.uint8)
    else:
        c = by_word.astype(ml_dtypes.float4_e2m1fn).view(np.uint8) & 0xF
        words = (c[..., 0::2] | (c[..., 1::2] << 4)).reshape(k // 512, 128, 2 * n)
    return np.ascontiguousarray(words), np.ascontiguousarray(byte.astype(np.uint8).reshape(k // 512, 16, n))


def unpack_weight(words, scales, fmt):
    g, _, n = scales.shape
    words = np.ascontiguousarray(words).reshape(g, 128, n, -1)
    if fmt == "e4m3":
        vals = words.view(ml_dtypes.float8_e4m3fn).astype(np.float64)
    else:
        nib = np.empty((g, 128, n, 4), np.uint8)
        nib[..., 0::2] = words & 0xF
        nib[..., 1::2] = words >> 4
        vals = E2M1[nib]
    vals = vals * np.repeat(np.exp2(scales.astype(np.float64) - 127.0), 8, axis=1)[..., None]
    return vals.transpose(0, 1, 3, 2).reshape(g * 512, n)


def gelu(v):
    return 0.5 * v * (1.0 + np.tanh(np.sqrt(2.0 / np.pi) * (v + 0.044715 * v**3)))


def often(T, S):
    return np.random.permutation(T)[(T * np.random.uniform(0, 1, S) ** 4).astype(np.int64)]


K, K2, H, T, S, P = 1024, 512, 1024, 4096, 1024, 512

def setup_inputs():
    n = np.random.standard_normal
    s, s2, u = mx_kscale(K)[:, None], mx_kscale(K2)[:, None], mx_kscale(H)[:, None]
    d = {}
    d["tab_words"], d["tab_scales"] = pack_weight(n((K, T)) * s, "e4m3")
    d["tab2_words"], d["tab2_scales"] = pack_weight(n((K2, T)) * s2, "e4m3")
    d["tab3_words"], d["tab3_scales"] = pack_weight(n((K2, T)) * s2, "e4m3")
    d["offs"] = striped(np.random.permutation(T)[:S])
    d["offs2"] = striped(np.random.permutation(T)[:S])
    d["offs3"] = striped(np.random.permutation(T)[:S])
    d["pos1"] = striped(np.random.permutation(S)[:P])
    d["pos2"] = striped(often(S, P))
    d["pos3"] = striped(often(S, P))
    d["w1"] = (n((K, H)) / s * u.T / K ** 0.5).astype(np.float32)
    d["w2_words"], d["w2_scales"] = pack_weight(1.6 * n((K2, H)) / s2 / K2 ** 0.5, "e2m1")
    d["w3"] = (n((K2, H)) / s2 * u.T / K2 ** 0.5).astype(np.float32)
    d["w4_words"], d["w4_scales"] = pack_weight(n((H, H)) / u / H ** 0.5, "e4m3")
    d["gb"] = (np.exp(0.3 * n(H)) * u[:, 0]).astype(np.float32)
    d["ga"] = (np.exp(0.3 * n(H)) / u[:, 0]).astype(np.float32)
    return d

def reference(tab_words, tab_scales, tab2_words, tab2_scales, tab3_words, tab3_scales,
              offs, offs2, offs3, pos1, pos2, pos3, w1, w2_words, w2_scales, w3,
              w4_words, w4_scales, gb, ga):
    v = unpack_weight(tab_words, tab_scales, "e4m3")[:, unstriped(offs)]
    v2 = unpack_weight(tab2_words, tab2_scales, "e4m3")[:, unstriped(offs2)]
    v3 = unpack_weight(tab3_words, tab3_scales, "e4m3")[:, unstriped(offs3)]
    a = mxq(f64(w1), 0, "e4m3").T @ v
    e = unpack_weight(w2_words, w2_scales, "e2m1").T @ v2
    b = f64(gb)[:, None] * (0.5 * e * (1.0 + np.tanh(0.7978845608 * (e + 0.044715 * e ** 3))))
    d = mxq(f64(w3), 0, "e4m3").T @ v3
    xa = a[:, unstriped(pos1)]
    z = xa - b[:, unstriped(pos2)] + d[:, unstriped(pos3)]
    y = unpack_weight(w4_words, w4_scales, "e4m3").T @ mxq(z, 0, "e4m3")
    return np.abs(y - f64(ga)[:, None] * xa)

@@ -1,0 +1,279 @@
+from contextlib import ExitStack
+
+import concourse.mybir as mybir
+from concourse.masks import make_identity
+
+K, K2, H, T, S, J = 1024, 512, 1024, 4096, 1024, 512
+FLOPS = 2 * (K * H * S + 2 * K2 * H * S + H * H * J)
+
+F32 = mybir.dt.float32
+BF16 = mybir.dt.bfloat16
+I32 = mybir.dt.int32
+U32 = mybir.dt.uint32
+U16 = mybir.dt.uint16
+U8 = mybir.dt.uint8
+FP8X4 = mybir.dt.float8_e4m3fn_x4
+FP4X4 = mybir.dt.float4_e2m1fn_x4
+ALU = mybir.AluOpType
+ACT = mybir.ActivationFunctionType
+
+P = 128
+KIB = 1024
+NB = 512
+SLICES = H // P
+
+
+def tile_list_payslip_discrepancy_features_kernel(
+    tc, tab_words, tab_scales, tab2_words, tab2_scales, tab3_words, tab3_scales,
+    offs, offs2, offs3, pos1, pos2, pos3, w1, w2_words, w2_scales, w3,
+    w4_words, w4_scales, gb, ga, out,
+):
+    nc = tc.nc
+    with ExitStack() as ctx:
+        keep = ctx.enter_context(tc.tile_pool(name="keep", bufs=1))
+        ring = ctx.enter_context(tc.tile_pool(name="ring", bufs=1))
+        arena = ctx.enter_context(tc.tile_pool(name="arena", bufs=1))
+        psum = ctx.enter_context(tc.psum_pool(name="psum", bufs=1))
+
+        def load_list(src, name):
+            lst = keep.tile(list(src.shape), U16, name=name)
+            nc.sync.dma_start(lst[:], src)
+            return lst
+
+        def placed(shape, dtype, name, kib):
+            return arena.tile(shape, dtype, name=name, align_bytes=64, offset=kib * KIB)
+
+        def zeroed_plane(width, name, engine, kib):
+            plane = placed([P, width], U8, name, kib)
+            engine.memset(plane[:].bitcast(I32), 0)
+            return plane
+
+        def load_scale_rows(plane, src, queue):
+            passes = src.shape[0]
+            for q in range(4):
+                queue.dma_start(
+                    out=plane[32 * q : 32 * q + 4 * passes, :].bitcast(I32),
+                    in_=src[:, 4 * q : 4 * q + 4, :].bitcast(I32),
+                )
+
+        def load_table(words, a, name, kib):
+            win = placed([P, T], I32, name, kib)
+            nc.sync.dma_start(out=win[:], in_=words[a].rearrange("p t i -> p (t i)").bitcast(I32))
+            return win
+
+        def pick_words(win, lst, name, kib):
+            got = placed([P, S], U32, name, kib)
+            nc.vector.tensor_copy(got[:], win[:].bitcast(U32).indirect(lst[:]))
+            return got
+
+        def pick_scales(plane, lst, name, kib):
+            got = placed([P, S], U8, name, kib)
+            nc.vector.tensor_copy(got[:], plane[:].indirect(lst[:]))
+            return got
+
+        def load_weight(w, a, h, name, kib):
+            raw = placed([P, 4, NB], F32, name, kib)
+            rows = w[512 * a : 512 * (a + 1), NB * h : NB * (h + 1)]
+            nc.sync.dma_start(out=raw[:], in_=rows.rearrange("(p i) c -> p i c", i=4))
+            return raw
+
+        def quantise(grouped, name):
+            codes = keep.tile([P, NB], U32, name=name + "_codes", align_bytes=64)
+            scales = keep.tile([P, NB], U8, name=name + "_scales", align_bytes=64)
+            nc.vector.quantize_mx(
+                out=codes[:].bitcast(FP8X4), scales=scales[:],
+                in_=grouped[:].rearrange("p c i -> p (c i)"),
+            )
+            return codes, scales
+
+        def quantise_weight(raw, name, kib):
+            grouped = placed([P, NB, 4], BF16, name + "_grouped", kib)
+            nc.scalar.copy(
+                out=grouped[:].rearrange("p (c n) i -> p c i n", n=4),
+                in_=raw[:].rearrange("p i (c n) -> p c i n", n=4),
+            )
+            return quantise(grouped, name)
+
+        def first_stage(stationary, moving, func):
+            win = ring.tile([P, S], F32, name="win", tag="win", bufs=10)
+            for h in range(S // NB):
+                cols = slice(NB * h, NB * (h + 1))
+                acc = psum.tile([P, NB], F32, name="acc", tag="acc", bufs=4)
+                for a, ((lw, ls), (rw, rs)) in enumerate(zip(stationary, moving)):
+                    nc.tensor.matmul_mx(
+                        out=acc[:], lhsT=lw, lhsT_scale=ls,
+                        rhs=rw[:, cols].bitcast(FP8X4), rhs_scale=rs[:, cols],
+                        start=(a == 0), stop=(a == len(moving) - 1),
+                    )
+                if func is None:
+                    nc.scalar.copy(out=win[:, cols], in_=acc[:])
+                else:
+                    nc.scalar.activation(out=win[:, cols], in_=acc[:], func=func)
+            return win
+
+        v2_plane = zeroed_plane(T, "v2_plane", nc.vector, 72)
+        v_plane = zeroed_plane(T, "v_plane", nc.vector, 48)
+        v3_plane = zeroed_plane(T, "v3_plane", nc.vector, 44)
+        ident = keep.tile([P, P], F32, name="ident")
+        make_identity(nc, ident[:])
+        gains_rows = arena.tile([P, P], F32, name="gains_rows", align_bytes=64, offset=24 * KIB - 256)
+        nc.gpsimd.memset(gains_rows[:], 0.0)
+        nc.gpsimd.dma_start(out=gains_rows[0:SLICES, :], in_=gb.rearrange("(s p) -> s p", p=P))
+        nc.gpsimd.dma_start(out=gains_rows[SLICES : 2 * SLICES, :], in_=ga.rearrange("(s p) -> s p", p=P))
+        w2_plane = zeroed_plane(H, "w2_plane", nc.gpsimd, 76)
+        load_scale_rows(w2_plane, w2_scales, nc.gpsimd)
+
+        l_offs2 = load_list(offs2, "l_offs2")
+        l_offs = load_list(offs, "l_offs")
+        l_offs3 = load_list(offs3, "l_offs3")
+        l_pos2 = load_list(pos2, "l_pos2")
+        l_pos1 = load_list(pos1, "l_pos1")
+        l_pos3 = load_list(pos3, "l_pos3")
+        w2_codes = placed([P, 2 * H], U8, "w2_codes", 106)
+        nc.sync.dma_start(out=w2_codes[:].bitcast(I32), in_=w2_words[0].bitcast(I32))
+        v2_win = load_table(tab2_words, 0, "v2_win", 0)
+        load_scale_rows(v2_plane, tab2_scales, nc.scalar)
+        load_scale_rows(v_plane, tab_scales, nc.scalar)
+        load_scale_rows(v3_plane, tab3_scales, nc.scalar)
+
+        gains_t = psum.tile([P, P], F32, name="gains_t", tag="turn", bufs=2)
+        nc.tensor.transpose(gains_t[:], gains_rows[:], ident[:])
+        gains = keep.tile([P, 2 * SLICES], F32, name="gains")
+        nc.scalar.copy(out=gains[:], in_=gains_t[:, 0 : 2 * SLICES])
+
+        neg_b = []
+        xa = []
+        xd = []
+
+        def pick_agreements(s, kib):
+            stationary = [(w2_codes[:, 2 * P * s : 2 * P * (s + 1)].bitcast(FP4X4), w2_plane[:, P * s : P * (s + 1)])]
+            win = first_stage(stationary, [(v2_w, v2_s)], ACT.Gelu_apprx_tanh)
+            got = placed([P, J], F32, "neg_b%d" % s, kib)
+            nc.vector.tensor_copy(got[:], win[:].indirect(l_pos2[:]))
+            nc.vector.tensor_scalar(got[:], got[:], gains[:, s : s + 1], -1.0, ALU.mult, ALU.mult)
+            neg_b.append(got)
+
+        def pick_payslips(s, kib):
+            h, c = divmod(s, 4)
+            cols = slice(P * c, P * (c + 1))
+            stationary = [(w1_q[a, h][0][:, cols].bitcast(FP8X4), w1_q[a, h][1][:, cols]) for a in range(2)]
+            moving = [(v_w[a], v_s[4 * a :, :]) for a in range(2)]
+            win = first_stage(stationary, moving, None)
+            got = placed([P, J], F32, "xa%d" % s, kib)
+            nc.vector.tensor_copy(got[:], win[:].indirect(l_pos1[:]))
+            xa.append(got)
+
+        def pick_absences(s):
+            h, c = divmod(s, 4)
+            cols = slice(P * c, P * (c + 1))
+            stationary = [(w3_q[h][0][:, cols].bitcast(FP8X4), w3_q[h][1][:, cols])]
+            win = first_stage(stationary, [(v3_w, v3_s)], None)
+            got = ring.tile([P, J], F32, name="xd", tag="xd", bufs=6)
+            nc.vector.tensor_copy(got[:], win[:].indirect(l_pos3[:]))
+            xd.append(got)
+
+        w1_q = {}
+        w1_00 = load_weight(w1, 0, 0, "w1_00", 16)
+        v_win0 = load_table(tab_words, 0, "v_win0", 24)
+        v2_s = pick_scales(v2_plane, l_offs2, "v2_s", 77)
+        v2_w = pick_words(v2_win, l_offs2, "v2_w", 72)
+        w1_10 = load_weight(w1, 1, 0, "w1_10", 0)
+        v_s = pick_scales(v_plane, l_offs, "v_s", 8)
+        v_win1 = load_table(tab_words, 1, "v_win1", 48)
+        w1_q[0, 0] = quantise_weight(w1_00, "w1q_00", 88)
+        w1_01 = load_weight(w1, 0, 1, "w1_01", 16)
+        v3_s = pick_scales(v3_plane, l_offs3, "v3_s", 9)
+        pick_agreements(0, 78)
+        v_w = [pick_words(v_win0, l_offs, "v_w0", 12)]
+        v3_win = load_table(tab3_words, 0, "v3_win", 28)
+        pick_agreements(1, 24)
+        pick_agreements(2, 26)
+        w1_q[1, 0] = quantise_weight(w1_10, "w1q_10", 92)
+        w1_11 = load_weight(w1, 1, 1, "w1_11", 0)
+        v_w.append(pick_words(v_win1, l_offs, "v_w1", 80))
+        w3_0 = load_weight(w3, 0, 0, "w3_0", 52)
+        w3_1 = load_weight(w3, 0, 1, "w3_1", 60)
+        pick_agreements(3, 48)
+        pick_agreements(4, 50)
+        w1_q[0, 1] = quantise_weight(w1_01, "w1q_01", 88)
+        w4_codes = placed([P, 2, H], I32, "w4_codes", 16)
+        nc.sync.dma_start(out=w4_codes[:], in_=w4_words.rearrange("a p c i -> p a (c i)").bitcast(I32))
+        pick_agreements(5, 88)
+        pick_agreements(6, 90)
+        v3_w = pick_words(v3_win, l_offs3, "v3_w", 84)
+        w1_q[1, 1] = quantise_weight(w1_11, "w1q_11", 92)
+        w3_q = [quantise_weight(w3_0, "w3q_0", 96)]
+        pick_agreements(7, 96)
+        w4_plane = zeroed_plane(H, "w4_plane", nc.gpsimd, 76)
+        load_scale_rows(w4_plane, w4_scales, nc.sync)
+        w3_q.append(quantise_weight(w3_1, "w3q_1", 100))
+        pick_payslips(0, 100)
+        pick_payslips(1, 102)
+        pick_payslips(2, 28)
+        pick_payslips(3, 30)
+
+        z_rows = [keep.tile([P, 4, 2, P, 2], BF16, name="z_rows%d" % b) for b in range(2)]
+        z_q = []
+
+        def join(s):
+            b, c = divmod(s, 4)
+            bank = psum.tile([P, 4, P], F32, name="join", tag="join", bufs=2)
+            terms = [neg_b[s], xa[s], xd[s]]
+            for n, term in enumerate(terms):
+                for jb in range(4):
+                    nc.tensor.matmul(
+                        bank[:, jb, :], lhsT=term[:, P * jb : P * (jb + 1)], rhs=ident[:], is_transpose=True,
+                        start=(n == 0 and jb == 0), stop=(n == 2 and jb == 3),
+                    )
+            nc.scalar.copy(
+                out=z_rows[b][:, :, :, 32 * c : 32 * (c + 1), :],
+                in_=bank[:].rearrange("j g (q u e) -> j g u q e", u=2, e=2),
+            )
+
+        def quantise_z(b):
+            words = z_rows[b][:].rearrange("j g u p e -> j (g u p e)").bitcast(F32)
+            grouped = ring.tile([P, NB, 4], BF16, name="grouped", tag="grouped", bufs=2, align_bytes=64)
+            gwords = grouped[:].rearrange("p j i -> p (j i)").bitcast(F32)
+            for half in range(2):
+                bank = psum.tile([P, 4, P], F32, name="turn", tag="turn", bufs=2)
+                for gu in range(4):
+                    n = 4 * half + gu
+                    nc.tensor.transpose(bank[:, gu, :], words[:, P * n : P * (n + 1)], ident[:])
+                copy = nc.vector.tensor_copy if (b, half) == (1, 1) else nc.scalar.copy
+                copy(
+                    out=gwords[:, NB * half : NB * (half + 1)].rearrange("p (g j u) -> p g j u", g=2, u=2),
+                    in_=bank[:].rearrange("p (g u) j -> p g j u", u=2),
+                )
+            return quantise(grouped, "z_%d" % b)
+
+        d_lag, join_lag = 4, 2
+        for step in range(min(4, d_lag), SLICES + d_lag + join_lag):
+            if 4 <= step < SLICES:
+                pick_payslips(step, 24 + 2 * step)
+            if 0 <= step - d_lag < SLICES:
+                pick_absences(step - d_lag)
+            s = step - d_lag - join_lag
+            if s >= 0:
+                join(s)
+                if s % 4 == 3:
+                    z_q.append(quantise_z(s // 4))
+
+        for s in range(SLICES):
+            cols = slice(P * s, P * (s + 1))
+            if s in (4, 5):
+                acc = psum.tile([P, NB], F32, name="acc_y", tag="join", bufs=2)
+            else:
+                acc = psum.tile([P, NB], F32, name="acc", tag="acc", bufs=4)
+            for b in range(2):
+                nc.tensor.matmul_mx(
+                    out=acc[:], lhsT=w4_codes[:, b, cols].bitcast(FP8X4), lhsT_scale=w4_plane[4 * b :, cols],
+                    rhs=z_q[b][0][:].bitcast(FP8X4), rhs_scale=z_q[b][1][:],
+                    start=(b == 0), stop=(b == 1),
+                )
+            res = ring.tile([P, J], F32, name="res", tag="res", bufs=8)
+            nc.vector.scalar_tensor_tensor(
+                out=res[:], in0=xa[s][:], scalar=gains[:, SLICES + s : SLICES + s + 1], in1=acc[:],
+                op0=ALU.mult, op1=ALU.subtract,
+            )
+            nc.scalar.activation(out=res[:], in_=res[:], func=ACT.Abs)
+            nc.sync.dma_start(out=out[cols, :], in_=res[:])

@@ -20,6 +20,7 @@ ACT = mybir.ActivationFunctionType
 P = 128
 KIB = 1024
 NB = 512
+HALF = J // 2
 SLICES = H // P
 
 
@@ -48,10 +49,10 @@ def tile_list_payslip_discrepancy_features_kernel(
             engine.memset(plane[:].bitcast(I32), 0)
             return plane
 
-        def load_scale_rows(plane, src, queue):
+        def load_scale_rows(plane, src, quadrants):
             passes = src.shape[0]
-            for q in range(4):
-                queue.dma_start(
+            for q in quadrants:
+                nc.sync.dma_start(
                     out=plane[32 * q : 32 * q + 4 * passes, :].bitcast(I32),
                     in_=src[:, 4 * q : 4 * q + 4, :].bitcast(I32),
                 )
@@ -78,8 +79,9 @@ def tile_list_payslip_discrepancy_features_kernel(
             return raw
 
         def quantise(grouped, name):
-            codes = keep.tile([P, NB], U32, name=name + "_codes", align_bytes=64)
-            scales = keep.tile([P, NB], U8, name=name + "_scales", align_bytes=64)
+            width = grouped.shape[1]
+            codes = keep.tile([P, width], U32, name=name + "_codes", align_bytes=64)
+            scales = keep.tile([P, width], U8, name=name + "_scales", align_bytes=64)
             nc.vector.quantize_mx(
                 out=codes[:].bitcast(FP8X4), scales=scales[:],
                 in_=grouped[:].rearrange("p c i -> p (c i)"),
@@ -94,8 +96,11 @@ def tile_list_payslip_discrepancy_features_kernel(
             )
             return quantise(grouped, name)
 
-        def first_stage(stationary, moving, func):
-            win = ring.tile([P, S], F32, name="win", tag="win", bufs=10)
+        def first_stage(stationary, moving, func, name, kib=None):
+            if kib is None:
+                win = ring.tile([P, S], F32, name=name, tag="win", bufs=10)
+            else:
+                win = placed([P, S], F32, name, kib)
             for h in range(S // NB):
                 cols = slice(NB * h, NB * (h + 1))
                 acc = psum.tile([P, NB], F32, name="acc", tag="acc", bufs=4)
@@ -111,17 +116,14 @@ def tile_list_payslip_discrepancy_features_kernel(
                     nc.scalar.activation(out=win[:, cols], in_=acc[:], func=func)
             return win
 
+        gains_rows = keep.tile([P, P], F32, name="gains_rows")
+        nc.gpsimd.memset(gains_rows[:], 0.0)
         v2_plane = zeroed_plane(T, "v2_plane", nc.vector, 72)
         v_plane = zeroed_plane(T, "v_plane", nc.vector, 48)
         v3_plane = zeroed_plane(T, "v3_plane", nc.vector, 44)
+        w2_plane = zeroed_plane(H, "w2_plane", nc.gpsimd, 76)
         ident = keep.tile([P, P], F32, name="ident")
         make_identity(nc, ident[:])
-        gains_rows = arena.tile([P, P], F32, name="gains_rows", align_bytes=64, offset=24 * KIB - 256)
-        nc.gpsimd.memset(gains_rows[:], 0.0)
-        nc.gpsimd.dma_start(out=gains_rows[0:SLICES, :], in_=gb.rearrange("(s p) -> s p", p=P))
-        nc.gpsimd.dma_start(out=gains_rows[SLICES : 2 * SLICES, :], in_=ga.rearrange("(s p) -> s p", p=P))
-        w2_plane = zeroed_plane(H, "w2_plane", nc.gpsimd, 76)
-        load_scale_rows(w2_plane, w2_scales, nc.gpsimd)
 
         l_offs2 = load_list(offs2, "l_offs2")
         l_offs = load_list(offs, "l_offs")
@@ -129,151 +131,191 @@ def tile_list_payslip_discrepancy_features_kernel(
         l_pos2 = load_list(pos2, "l_pos2")
         l_pos1 = load_list(pos1, "l_pos1")
         l_pos3 = load_list(pos3, "l_pos3")
-        w2_codes = placed([P, 2 * H], U8, "w2_codes", 106)
-        nc.sync.dma_start(out=w2_codes[:].bitcast(I32), in_=w2_words[0].bitcast(I32))
+        w2_codes = [placed([P, H], U8, "w2_codes%d" % h, 106 + h) for h in range(2)]
+        for h in range(2):
+            nc.sync.dma_start(out=w2_codes[h][:].bitcast(I32), in_=w2_words[0, :, H * h : H * (h + 1)].bitcast(I32))
+        nc.sync.dma_start(out=gains_rows[0:SLICES, :], in_=gb.rearrange("(s p) -> s p", p=P))
+        load_scale_rows(v2_plane, tab2_scales, range(4))
         v2_win = load_table(tab2_words, 0, "v2_win", 0)
-        load_scale_rows(v2_plane, tab2_scales, nc.scalar)
-        load_scale_rows(v_plane, tab_scales, nc.scalar)
-        load_scale_rows(v3_plane, tab3_scales, nc.scalar)
+        load_scale_rows(w2_plane, w2_scales, range(4))
+        load_scale_rows(v_plane, tab_scales, range(2))
+        w1_00 = load_weight(w1, 0, 0, "w1_00", 16)
+        load_scale_rows(v_plane, tab_scales, range(2, 4))
+        nc.sync.dma_start(out=gains_rows[SLICES : 2 * SLICES, :], in_=ga.rearrange("(s p) -> s p", p=P))
+        v_win0 = load_table(tab_words, 0, "v_win0", 24)
+        load_scale_rows(v3_plane, tab3_scales, range(4))
 
         gains_t = psum.tile([P, P], F32, name="gains_t", tag="turn", bufs=2)
         nc.tensor.transpose(gains_t[:], gains_rows[:], ident[:])
         gains = keep.tile([P, 2 * SLICES], F32, name="gains")
         nc.scalar.copy(out=gains[:], in_=gains_t[:, 0 : 2 * SLICES])
 
-        neg_b = []
-        xa = []
-        xd = []
+        neg_b = {}
+        xa = {}
+        xd = {}
 
-        def pick_agreements(s, kib):
-            stationary = [(w2_codes[:, 2 * P * s : 2 * P * (s + 1)].bitcast(FP4X4), w2_plane[:, P * s : P * (s + 1)])]
-            win = first_stage(stationary, [(v2_w, v2_s)], ACT.Gelu_apprx_tanh)
-            got = placed([P, J], F32, "neg_b%d" % s, kib)
-            nc.vector.tensor_copy(got[:], win[:].indirect(l_pos2[:]))
-            nc.vector.tensor_scalar(got[:], got[:], gains[:, s : s + 1], -1.0, ALU.mult, ALU.mult)
-            neg_b.append(got)
+        def agreements(s):
+            h, c = divmod(s, 4)
+            stationary = [(w2_codes[h][:, 2 * P * c : 2 * P * (c + 1)].bitcast(FP4X4), w2_plane[:, P * s : P * (s + 1)])]
+            return first_stage(stationary, [(v2_w, v2_s)], ACT.Gelu_apprx_tanh, "e%d" % s)
 
-        def pick_payslips(s, kib):
+        def payslips(s, kib=None):
             h, c = divmod(s, 4)
             cols = slice(P * c, P * (c + 1))
             stationary = [(w1_q[a, h][0][:, cols].bitcast(FP8X4), w1_q[a, h][1][:, cols]) for a in range(2)]
             moving = [(v_w[a], v_s[4 * a :, :]) for a in range(2)]
-            win = first_stage(stationary, moving, None)
-            got = placed([P, J], F32, "xa%d" % s, kib)
-            nc.vector.tensor_copy(got[:], win[:].indirect(l_pos1[:]))
-            xa.append(got)
+            return first_stage(stationary, moving, None, "a%d" % s, kib)
 
-        def pick_absences(s):
+        def absences(s):
             h, c = divmod(s, 4)
             cols = slice(P * c, P * (c + 1))
             stationary = [(w3_q[h][0][:, cols].bitcast(FP8X4), w3_q[h][1][:, cols])]
-            win = first_stage(stationary, [(v3_w, v3_s)], None)
-            got = ring.tile([P, J], F32, name="xd", tag="xd", bufs=6)
-            nc.vector.tensor_copy(got[:], win[:].indirect(l_pos3[:]))
-            xd.append(got)
+            return first_stage(stationary, [(v3_w, v3_s)], None, "d%d" % s)
+
+        def pick(into, s, win, lst, got):
+            nc.vector.tensor_copy(got[:], win[:].indirect(lst[:]))
+            for h in range(2):
+                into[s, h] = got[:, HALF * h : HALF * (h + 1)]
+
+        def pick_half(into, s, h, win, lst, got):
+            nc.vector.tensor_copy(got[:], win[:].indirect(lst[:, 16 * h : 16 * (h + 1)]))
+            into[s, h] = got[:]
+
+        def pick_agreements(s, win, kib):
+            got = placed([P, J], F32, "neg_b%d" % s, kib)
+            pick(neg_b, s, win, l_pos2, got)
+            nc.gpsimd.tensor_scalar(got[:], got[:], gains[:, s : s + 1], -1.0, ALU.mult, ALU.mult)
+
+        def pick_payslips(s, kib, win_kib=None):
+            pick(xa, s, payslips(s, win_kib), l_pos1, placed([P, J], F32, "xa%d" % s, kib))
+
+        def pick_absences(s):
+            pick(xd, s, absences(s), l_pos3, ring.tile([P, J], F32, name="xd%d" % s, tag="xd", bufs=6))
+
+        z_rows = {
+            (b, h): keep.tile([P, 2, 2, P, 2], BF16, name="z_rows%d%d" % (b, h)) for b in range(2) for h in range(2)
+        }
+        z_q = {}
+
+        def join(s, halves, terms, copy=nc.scalar.copy):
+            b, c = divmod(s, 4)
+            bank = psum.tile([P, len(halves), 2, P], F32, name="join%d" % s, tag="join", bufs=2)
+            steps = [(term, i, h, g) for term in terms for i, h in enumerate(halves) for g in range(2)]
+            for n, (term, i, h, g) in enumerate(steps):
+                nc.tensor.matmul(
+                    bank[:, i, g, :], lhsT=term[s, h][:, P * g : P * (g + 1)], rhs=ident[:], is_transpose=True,
+                    start=(n == 0), stop=(n == len(steps) - 1),
+                )
+            if (s, halves[0]) in ():
+                copy = nc.vector.tensor_copy
+            for i, h in enumerate(halves):
+                copy(
+                    out=z_rows[b, h][:, :, :, 32 * c : 32 * (c + 1), :],
+                    in_=bank[:, i].rearrange("j g (q u e) -> j g u q e", u=2, e=2),
+                )
+
+        def quantise_z(b, h):
+            words = z_rows[b, h][:].rearrange("j g u p e -> j (g u p e)").bitcast(F32)
+            grouped = ring.tile([P, HALF, 4], BF16, name="z_grouped", tag="z_grouped", bufs=2, align_bytes=64)
+            bank = psum.tile([P, 4, P], F32, name="turn", tag="turn", bufs=2)
+            for n in range(4):
+                nc.tensor.transpose(bank[:, n, :], words[:, P * n : P * (n + 1)], ident[:])
+            copy = nc.vector.tensor_copy if (b, h) in () else nc.scalar.copy
+            copy(
+                out=grouped[:].rearrange("p j i -> p (j i)").bitcast(F32).rearrange("p (g j u) -> p g j u", g=2, u=2),
+                in_=bank[:].rearrange("p (g u) j -> p g j u", u=2),
+            )
+            z_q[b, h] = quantise(grouped, "z_%d%d" % (b, h))
+
+        def second_stage(h):
+            for pair in range(SLICES // 2):
+                acc = psum.tile([P, 2, HALF], F32, name="y", tag="acc", bufs=4)
+                for b in range(2):
+                    for i in range(2):
+                        cols = slice(P * (2 * pair + i), P * (2 * pair + i + 1))
+                        nc.tensor.matmul_mx(
+                            out=acc[:, i, :], lhsT=w4_codes[:, b, cols].bitcast(FP8X4),
+                            lhsT_scale=w4_plane[4 * b :, cols],
+                            rhs=z_q[b, h][0][:].bitcast(FP8X4), rhs_scale=z_q[b, h][1][:],
+                            start=(b, i) == (0, 0), stop=(b, i) == (1, 1),
+                        )
+                res = ring.tile([P, 2, HALF], F32, name="res", tag="res", bufs=8)
+                for i in range(2):
+                    s = 2 * pair + i
+                    nc.vector.scalar_tensor_tensor(
+                        out=res[:, i, :], in0=xa[s, h], scalar=gains[:, SLICES + s : SLICES + s + 1], in1=acc[:, i, :],
+                        op0=ALU.mult, op1=ALU.subtract,
+                    )
+                nc.scalar.activation(out=res[:], in_=res[:], func=ACT.Abs)
+                rows = out[2 * P * pair : 2 * P * (pair + 1), HALF * h : HALF * (h + 1)]
+                nc.sync.dma_start(out=rows.rearrange("(i p) j -> p i j", i=2), in_=res[:])
 
         w1_q = {}
-        w1_00 = load_weight(w1, 0, 0, "w1_00", 16)
-        v_win0 = load_table(tab_words, 0, "v_win0", 24)
         v2_s = pick_scales(v2_plane, l_offs2, "v2_s", 77)
-        v2_w = pick_words(v2_win, l_offs2, "v2_w", 72)
+        v2_w = placed([P, S], U32, "v2_w", 72)
+        for h in range(2):
+            nc.vector.tensor_copy(
+                v2_w[:, NB * h : NB * (h + 1)], v2_win[:].bitcast(U32).indirect(l_offs2[:, 32 * h : 32 * (h + 1)])
+            )
         w1_10 = load_weight(w1, 1, 0, "w1_10", 0)
         v_s = pick_scales(v_plane, l_offs, "v_s", 8)
         v_win1 = load_table(tab_words, 1, "v_win1", 48)
         w1_q[0, 0] = quantise_weight(w1_00, "w1q_00", 88)
-        w1_01 = load_weight(w1, 0, 1, "w1_01", 16)
-        v3_s = pick_scales(v3_plane, l_offs3, "v3_s", 9)
-        pick_agreements(0, 78)
+        w3_0 = load_weight(w3, 0, 0, "w3_0", 16)
+        pick_agreements(0, agreements(0), 78)
         v_w = [pick_words(v_win0, l_offs, "v_w0", 12)]
         v3_win = load_table(tab3_words, 0, "v3_win", 28)
-        pick_agreements(1, 24)
-        pick_agreements(2, 26)
+        pick_agreements(1, agreements(1), 24)
+        pick_agreements(2, agreements(2), 26)
         w1_q[1, 0] = quantise_weight(w1_10, "w1q_10", 92)
-        w1_11 = load_weight(w1, 1, 1, "w1_11", 0)
+        w1_01 = load_weight(w1, 0, 1, "w1_01", 0)
         v_w.append(pick_words(v_win1, l_offs, "v_w1", 80))
-        w3_0 = load_weight(w3, 0, 0, "w3_0", 52)
+        w1_11 = load_weight(w1, 1, 1, "w1_11", 52)
         w3_1 = load_weight(w3, 0, 1, "w3_1", 60)
-        pick_agreements(3, 48)
-        pick_agreements(4, 50)
-        w1_q[0, 1] = quantise_weight(w1_01, "w1q_01", 88)
-        w4_codes = placed([P, 2, H], I32, "w4_codes", 16)
-        nc.sync.dma_start(out=w4_codes[:], in_=w4_words.rearrange("a p c i -> p a (c i)").bitcast(I32))
-        pick_agreements(5, 88)
-        pick_agreements(6, 90)
-        v3_w = pick_words(v3_win, l_offs3, "v3_w", 84)
-        w1_q[1, 1] = quantise_weight(w1_11, "w1q_11", 92)
-        w3_q = [quantise_weight(w3_0, "w3q_0", 96)]
-        pick_agreements(7, 96)
+        v3_s = pick_scales(v3_plane, l_offs3, "v3_s", 50)
+        pick_agreements(3, agreements(3), 48)
+        pick_agreements(4, agreements(4), 104)
+        late = {s: agreements(s) for s in range(5, SLICES)}
         w4_plane = zeroed_plane(H, "w4_plane", nc.gpsimd, 76)
-        load_scale_rows(w4_plane, w4_scales, nc.sync)
+        load_scale_rows(w4_plane, w4_scales, range(4))
+        w3_q = [quantise_weight(w3_0, "w3q_0", 88)]
+        v3_w = pick_words(v3_win, l_offs3, "v3_w", 84)
+        both = (0, 1)
+        pick_payslips(0, 28, 16)
+        pick_payslips(1, 30)
+        pick_payslips(2, 32)
+        w1_q[0, 1] = quantise_weight(w1_01, "w1q_01", 92)
+        w4_codes = placed([P, 2, H], I32, "w4_codes", 0)
+        nc.sync.dma_start(out=w4_codes[:], in_=w4_words.rearrange("a p c i -> p a (c i)").bitcast(I32))
+        pick_agreements(5, late[5], 92)
+        pick_absences(0)
+        pick_absences(1)
+        pick_payslips(3, 34)
+        w1_q[1, 1] = quantise_weight(w1_11, "w1q_11", 96)
+        pick_agreements(6, late[6], 96)
+        pick_absences(2)
+        join(0, both, [xd, neg_b, xa])
+        pick_absences(3)
+        join(1, both, [xd, neg_b, xa])
         w3_q.append(quantise_weight(w3_1, "w3q_1", 100))
-        pick_payslips(0, 100)
-        pick_payslips(1, 102)
-        pick_payslips(2, 28)
-        pick_payslips(3, 30)
-
-        z_rows = [keep.tile([P, 4, 2, P, 2], BF16, name="z_rows%d" % b) for b in range(2)]
-        z_q = []
-
-        def join(s):
-            b, c = divmod(s, 4)
-            bank = psum.tile([P, 4, P], F32, name="join", tag="join", bufs=2)
-            terms = [neg_b[s], xa[s], xd[s]]
-            for n, term in enumerate(terms):
-                for jb in range(4):
-                    nc.tensor.matmul(
-                        bank[:, jb, :], lhsT=term[:, P * jb : P * (jb + 1)], rhs=ident[:], is_transpose=True,
-                        start=(n == 0 and jb == 0), stop=(n == 2 and jb == 3),
-                    )
-            nc.scalar.copy(
-                out=z_rows[b][:, :, :, 32 * c : 32 * (c + 1), :],
-                in_=bank[:].rearrange("j g (q u e) -> j g u q e", u=2, e=2),
-            )
-
-        def quantise_z(b):
-            words = z_rows[b][:].rearrange("j g u p e -> j (g u p e)").bitcast(F32)
-            grouped = ring.tile([P, NB, 4], BF16, name="grouped", tag="grouped", bufs=2, align_bytes=64)
-            gwords = grouped[:].rearrange("p j i -> p (j i)").bitcast(F32)
-            for half in range(2):
-                bank = psum.tile([P, 4, P], F32, name="turn", tag="turn", bufs=2)
-                for gu in range(4):
-                    n = 4 * half + gu
-                    nc.tensor.transpose(bank[:, gu, :], words[:, P * n : P * (n + 1)], ident[:])
-                copy = nc.vector.tensor_copy if (b, half) == (1, 1) else nc.scalar.copy
-                copy(
-                    out=gwords[:, NB * half : NB * (half + 1)].rearrange("p (g j u) -> p g j u", g=2, u=2),
-                    in_=bank[:].rearrange("p (g u) j -> p g j u", u=2),
-                )
-            return quantise(grouped, "z_%d" % b)
-
-        d_lag, join_lag = 4, 2
-        for step in range(min(4, d_lag), SLICES + d_lag + join_lag):
-            if 4 <= step < SLICES:
-                pick_payslips(step, 24 + 2 * step)
-            if 0 <= step - d_lag < SLICES:
-                pick_absences(step - d_lag)
-            s = step - d_lag - join_lag
-            if s >= 0:
-                join(s)
-                if s % 4 == 3:
-                    z_q.append(quantise_z(s // 4))
-
-        for s in range(SLICES):
-            cols = slice(P * s, P * (s + 1))
-            if s in (4, 5):
-                acc = psum.tile([P, NB], F32, name="acc_y", tag="join", bufs=2)
-            else:
-                acc = psum.tile([P, NB], F32, name="acc", tag="acc", bufs=4)
-            for b in range(2):
-                nc.tensor.matmul_mx(
-                    out=acc[:], lhsT=w4_codes[:, b, cols].bitcast(FP8X4), lhsT_scale=w4_plane[4 * b :, cols],
-                    rhs=z_q[b][0][:].bitcast(FP8X4), rhs_scale=z_q[b][1][:],
-                    start=(b == 0), stop=(b == 1),
-                )
-            res = ring.tile([P, J], F32, name="res", tag="res", bufs=8)
-            nc.vector.scalar_tensor_tensor(
-                out=res[:], in0=xa[s][:], scalar=gains[:, SLICES + s : SLICES + s + 1], in1=acc[:],
-                op0=ALU.mult, op1=ALU.subtract,
-            )
-            nc.scalar.activation(out=res[:], in_=res[:], func=ACT.Abs)
-            nc.sync.dma_start(out=out[cols, :], in_=res[:])
+        pick_agreements(7, late[7], 100)
+        pick_payslips(4, 36)
+        join(2, both, [neg_b, xa, xd])
+        pick_absences(4)
+        join(3, both, [neg_b, xa, xd])
+        pick_payslips(5, 38)
+        pick_absences(5)
+        quantise_z(0, 0)
+        quantise_z(0, 1)
+        join(4, both, [neg_b, xa, xd])
+        pick_payslips(6, 40)
+        pick_absences(6)
+        join(5, both, [neg_b, xa, xd])
+        pick_payslips(7, 42)
+        pick_absences(7)
+        join(6, both, [neg_b, xa, xd])
+        join(7, both, [neg_b, xa, xd])
+        quantise_z(1, 0)
+        quantise_z(1, 1)
+        second_stage(0)
+        second_stage(1)

@@ -57,6 +57,21 @@ def tile_list_payslip_discrepancy_features_kernel(
                     in_=src[:, 4 * q : 4 * q + 4, :].bitcast(I32),
                 )
 
+        def scale_window(src, name, kib):
+            first = P - 16 * src.shape[0]
+            win = placed([P, T], U8, name, kib)
+            nc.vector.memset(win[0:first, :].bitcast(I32), 0)
+            nc.sync.dma_start(out=win[first:, :].bitcast(I32), in_=src.rearrange("a q t -> (a q) t").bitcast(I32))
+            return win
+
+        def move_scale_rows(plane, got, passes, a, quadrants):
+            for q in quadrants:
+                row = P - 16 * passes + 16 * a + 4 * q
+                nc.sync.dma_start(
+                    out=plane[32 * q + 4 * a : 32 * q + 4 * a + 4, :].bitcast(I32),
+                    in_=got[row : row + 4, :].bitcast(I32),
+                )
+
         def load_table(words, a, name, kib):
             win = placed([P, T], I32, name, kib)
             nc.sync.dma_start(out=win[:], in_=words[a].rearrange("p t i -> p (t i)").bitcast(I32))
@@ -90,7 +105,8 @@ def tile_list_payslip_discrepancy_features_kernel(
 
         def quantise_weight(raw, name, kib):
             grouped = placed([P, NB, 4], BF16, name + "_grouped", kib)
-            nc.scalar.copy(
+            copy = nc.vector.tensor_copy if name in () else nc.scalar.copy
+            copy(
                 out=grouped[:].rearrange("p (c n) i -> p c i n", n=4),
                 in_=raw[:].rearrange("p i (c n) -> p c i n", n=4),
             )
@@ -116,34 +132,36 @@ def tile_list_payslip_discrepancy_features_kernel(
                     nc.scalar.activation(out=win[:, cols], in_=acc[:], func=func)
             return win
 
-        gains_rows = keep.tile([P, P], F32, name="gains_rows")
-        nc.gpsimd.memset(gains_rows[:], 0.0)
-        v2_plane = zeroed_plane(T, "v2_plane", nc.vector, 72)
-        v_plane = zeroed_plane(T, "v_plane", nc.vector, 48)
-        v3_plane = zeroed_plane(T, "v3_plane", nc.vector, 44)
-        w2_plane = zeroed_plane(H, "w2_plane", nc.gpsimd, 76)
-        ident = keep.tile([P, P], F32, name="ident")
-        make_identity(nc, ident[:])
-
         l_offs2 = load_list(offs2, "l_offs2")
+        v2_rows = scale_window(tab2_scales, "v2_rows", 24)
         l_offs = load_list(offs, "l_offs")
-        l_offs3 = load_list(offs3, "l_offs3")
+        v_rows = scale_window(tab_scales, "v_rows", 48)
         l_pos2 = load_list(pos2, "l_pos2")
         l_pos1 = load_list(pos1, "l_pos1")
         l_pos3 = load_list(pos3, "l_pos3")
-        w2_codes = [placed([P, H], U8, "w2_codes%d" % h, 106 + h) for h in range(2)]
-        for h in range(2):
-            nc.sync.dma_start(out=w2_codes[h][:].bitcast(I32), in_=w2_words[0, :, H * h : H * (h + 1)].bitcast(I32))
-        nc.sync.dma_start(out=gains_rows[0:SLICES, :], in_=gb.rearrange("(s p) -> s p", p=P))
-        load_scale_rows(v2_plane, tab2_scales, range(4))
         v2_win = load_table(tab2_words, 0, "v2_win", 0)
-        load_scale_rows(w2_plane, w2_scales, range(4))
-        load_scale_rows(v_plane, tab_scales, range(2))
+        l_offs3 = load_list(offs3, "l_offs3")
+        w2_plane = zeroed_plane(H, "w2_plane", nc.gpsimd, 76)
+        v2_s = zeroed_plane(S, "v2_s", nc.gpsimd, 77)
+        v3_rows = scale_window(tab3_scales, "v3_rows", 44)
+        w2_codes = placed([P, 2 * H], U8, "w2_codes", 106)
+        nc.sync.dma_start(out=w2_codes[:].bitcast(I32), in_=w2_words[0].bitcast(I32))
+        load_scale_rows(w2_plane, w2_scales, range(3))
         w1_00 = load_weight(w1, 0, 0, "w1_00", 16)
-        load_scale_rows(v_plane, tab_scales, range(2, 4))
-        nc.sync.dma_start(out=gains_rows[SLICES : 2 * SLICES, :], in_=ga.rearrange("(s p) -> s p", p=P))
+        load_scale_rows(w2_plane, w2_scales, range(3, 4))
+        gains_rows = keep.tile([P, P], F32, name="gains_rows")
+        nc.gpsimd.memset(gains_rows[:], 0.0)
+        v_s = zeroed_plane(S, "v_s", nc.gpsimd, 108)
+        v3_s = zeroed_plane(S, "v3_s", nc.gpsimd, 109)
+        ident = keep.tile([P, P], F32, name="ident")
+        make_identity(nc, ident[:])
+
+        v2_got = pick_scales(v2_rows, l_offs2, "v2_got", 110)
+        move_scale_rows(v2_s, v2_got, 1, 0, range(4))
         v_win0 = load_table(tab_words, 0, "v_win0", 24)
-        load_scale_rows(v3_plane, tab3_scales, range(4))
+        nc.sync.dma_start(out=gains_rows[0:SLICES, :], in_=gb.rearrange("(s p) -> s p", p=P))
+        nc.sync.dma_start(out=gains_rows[SLICES : 2 * SLICES, :], in_=ga.rearrange("(s p) -> s p", p=P))
+        v_got = pick_scales(v_rows, l_offs, "v_got", 111)
 
         gains_t = psum.tile([P, P], F32, name="gains_t", tag="turn", bufs=2)
         nc.tensor.transpose(gains_t[:], gains_rows[:], ident[:])
@@ -155,8 +173,7 @@ def tile_list_payslip_discrepancy_features_kernel(
         xd = {}
 
         def agreements(s):
-            h, c = divmod(s, 4)
-            stationary = [(w2_codes[h][:, 2 * P * c : 2 * P * (c + 1)].bitcast(FP4X4), w2_plane[:, P * s : P * (s + 1)])]
+            stationary = [(w2_codes[:, 2 * P * s : 2 * P * (s + 1)].bitcast(FP4X4), w2_plane[:, P * s : P * (s + 1)])]
             return first_stage(stationary, [(v2_w, v2_s)], ACT.Gelu_apprx_tanh, "e%d" % s)
 
         def payslips(s, kib=None):
@@ -184,7 +201,7 @@ def tile_list_payslip_discrepancy_features_kernel(
         def pick_agreements(s, win, kib):
             got = placed([P, J], F32, "neg_b%d" % s, kib)
             pick(neg_b, s, win, l_pos2, got)
-            nc.gpsimd.tensor_scalar(got[:], got[:], gains[:, s : s + 1], -1.0, ALU.mult, ALU.mult)
+            nc.vector.tensor_scalar(got[:], got[:], gains[:, s : s + 1], -1.0, ALU.mult, ALU.mult)
 
         def pick_payslips(s, kib, win_kib=None):
             pick(xa, s, payslips(s, win_kib), l_pos1, placed([P, J], F32, "xa%d" % s, kib))
@@ -206,7 +223,7 @@ def tile_list_payslip_discrepancy_features_kernel(
                     bank[:, i, g, :], lhsT=term[s, h][:, P * g : P * (g + 1)], rhs=ident[:], is_transpose=True,
                     start=(n == 0), stop=(n == len(steps) - 1),
                 )
-            if (s, halves[0]) in ():
+            if (s, halves[0]) in ((5,0),(6,0),(7,1)):
                 copy = nc.vector.tensor_copy
             for i, h in enumerate(halves):
                 copy(
@@ -220,7 +237,7 @@ def tile_list_payslip_discrepancy_features_kernel(
             bank = psum.tile([P, 4, P], F32, name="turn", tag="turn", bufs=2)
             for n in range(4):
                 nc.tensor.transpose(bank[:, n, :], words[:, P * n : P * (n + 1)], ident[:])
-            copy = nc.vector.tensor_copy if (b, h) in () else nc.scalar.copy
+            copy = nc.vector.tensor_copy if (b, h) in ((0,1),(1,1)) else nc.scalar.copy
             copy(
                 out=grouped[:].rearrange("p j i -> p (j i)").bitcast(F32).rearrange("p (g j u) -> p g j u", g=2, u=2),
                 in_=bank[:].rearrange("p (g u) j -> p g j u", u=2),
@@ -246,25 +263,30 @@ def tile_list_payslip_discrepancy_features_kernel(
                         out=res[:, i, :], in0=xa[s, h], scalar=gains[:, SLICES + s : SLICES + s + 1], in1=acc[:, i, :],
                         op0=ALU.mult, op1=ALU.subtract,
                     )
-                nc.scalar.activation(out=res[:], in_=res[:], func=ACT.Abs)
-                rows = out[2 * P * pair : 2 * P * (pair + 1), HALF * h : HALF * (h + 1)]
-                nc.sync.dma_start(out=rows.rearrange("(i p) j -> p i j", i=2), in_=res[:])
+                rows = out[2 * P * pair : 2 * P * (pair + 1), HALF * h : HALF * (h + 1)].rearrange("(i p) j -> p i j", i=2)
+                last = h == 1 and pair == SLICES // 2 - 1
+                for part in [slice(0, 1), slice(1, 2)] if last else [slice(0, 2)]:
+                    nc.scalar.activation(out=res[:, part, :], in_=res[:, part, :], func=ACT.Abs)
+                    nc.sync.dma_start(out=rows[:, part, :], in_=res[:, part, :])
 
         w1_q = {}
-        v2_s = pick_scales(v2_plane, l_offs2, "v2_s", 77)
         v2_w = placed([P, S], U32, "v2_w", 72)
         for h in range(2):
             nc.vector.tensor_copy(
                 v2_w[:, NB * h : NB * (h + 1)], v2_win[:].bitcast(U32).indirect(l_offs2[:, 32 * h : 32 * (h + 1)])
             )
         w1_10 = load_weight(w1, 1, 0, "w1_10", 0)
-        v_s = pick_scales(v_plane, l_offs, "v_s", 8)
         v_win1 = load_table(tab_words, 1, "v_win1", 48)
+        v3_got = pick_scales(v3_rows, l_offs3, "v3_got", 8)
+        move_scale_rows(v_s, v_got, 2, 0, range(3))
         w1_q[0, 0] = quantise_weight(w1_00, "w1q_00", 88)
         w3_0 = load_weight(w3, 0, 0, "w3_0", 16)
+        move_scale_rows(v_s, v_got, 2, 0, range(3, 4))
+        move_scale_rows(v_s, v_got, 2, 1, range(4))
         pick_agreements(0, agreements(0), 78)
         v_w = [pick_words(v_win0, l_offs, "v_w0", 12)]
         v3_win = load_table(tab3_words, 0, "v3_win", 28)
+        move_scale_rows(v3_s, v3_got, 1, 0, range(4))
         pick_agreements(1, agreements(1), 24)
         pick_agreements(2, agreements(2), 26)
         w1_q[1, 0] = quantise_weight(w1_10, "w1q_10", 92)
@@ -272,7 +294,6 @@ def tile_list_payslip_discrepancy_features_kernel(
         v_w.append(pick_words(v_win1, l_offs, "v_w1", 80))
         w1_11 = load_weight(w1, 1, 1, "w1_11", 52)
         w3_1 = load_weight(w3, 0, 1, "w3_1", 60)
-        v3_s = pick_scales(v3_plane, l_offs3, "v3_s", 50)
         pick_agreements(3, agreements(3), 48)
         pick_agreements(4, agreements(4), 104)
         late = {s: agreements(s) for s in range(5, SLICES)}
@@ -312,9 +333,11 @@ def tile_list_payslip_discrepancy_features_kernel(
         pick_absences(6)
         join(5, both, [neg_b, xa, xd])
         pick_payslips(7, 42)
-        pick_absences(7)
+        d_last = absences(7)
         join(6, both, [neg_b, xa, xd])
-        join(7, both, [neg_b, xa, xd])
+        for h in range(2):
+            pick_half(xd, 7, h, d_last, l_pos3, ring.tile([P, HALF], F32, name="xd7%d" % h, tag="xd", bufs=6))
+            join(7, (h,), [neg_b, xa, xd])
         quantise_z(1, 0)
         quantise_z(1, 1)
         second_stage(0)

@@ -107,8 +107,8 @@ def tile_list_payslip_discrepancy_features_kernel(
             grouped = placed([P, NB, 4], BF16, name + "_grouped", kib)
             copy = nc.vector.tensor_copy if name in () else nc.scalar.copy
             copy(
-                out=grouped[:].rearrange("p (c n) i -> p c i n", n=4),
-                in_=raw[:].rearrange("p i (c n) -> p c i n", n=4),
+                out=grouped[:].rearrange("p (c n) (u e) -> p c u n e", n=4, e=2),
+                in_=raw[:].rearrange("p (u e) (c n) -> p c u n e", n=4, e=2),
             )
             return quantise(grouped, name)
 
@@ -223,7 +223,7 @@ def tile_list_payslip_discrepancy_features_kernel(
                     bank[:, i, g, :], lhsT=term[s, h][:, P * g : P * (g + 1)], rhs=ident[:], is_transpose=True,
                     start=(n == 0), stop=(n == len(steps) - 1),
                 )
-            if (s, halves[0]) in ((5,0),(6,0),(7,1)):
+            if (s, halves[0]) in ():
                 copy = nc.vector.tensor_copy
             for i, h in enumerate(halves):
                 copy(
@@ -237,7 +237,7 @@ def tile_list_payslip_discrepancy_features_kernel(
             bank = psum.tile([P, 4, P], F32, name="turn", tag="turn", bufs=2)
             for n in range(4):
                 nc.tensor.transpose(bank[:, n, :], words[:, P * n : P * (n + 1)], ident[:])
-            copy = nc.vector.tensor_copy if (b, h) in ((0,1),(1,1)) else nc.scalar.copy
+            copy = nc.vector.tensor_copy if (b, h) in () else nc.scalar.copy
             copy(
                 out=grouped[:].rearrange("p j i -> p (j i)").bitcast(F32).rearrange("p (g j u) -> p g j u", g=2, u=2),
                 in_=bank[:].rearrange("p (g u) j -> p g j u", u=2),
@@ -263,11 +263,9 @@ def tile_list_payslip_discrepancy_features_kernel(
                         out=res[:, i, :], in0=xa[s, h], scalar=gains[:, SLICES + s : SLICES + s + 1], in1=acc[:, i, :],
                         op0=ALU.mult, op1=ALU.subtract,
                     )
-                rows = out[2 * P * pair : 2 * P * (pair + 1), HALF * h : HALF * (h + 1)].rearrange("(i p) j -> p i j", i=2)
-                last = h == 1 and pair == SLICES // 2 - 1
-                for part in [slice(0, 1), slice(1, 2)] if last else [slice(0, 2)]:
-                    nc.scalar.activation(out=res[:, part, :], in_=res[:, part, :], func=ACT.Abs)
-                    nc.sync.dma_start(out=rows[:, part, :], in_=res[:, part, :])
+                nc.scalar.activation(out=res[:], in_=res[:], func=ACT.Abs)
+                rows = out[2 * P * pair : 2 * P * (pair + 1), HALF * h : HALF * (h + 1)]
+                nc.sync.dma_start(out=rows.rearrange("(i p) j -> p i j", i=2), in_=res[:])
 
         w1_q = {}
         v2_w = placed([P, S], U32, "v2_w", 72)
@@ -333,11 +331,9 @@ def tile_list_payslip_discrepancy_features_kernel(
         pick_absences(6)
         join(5, both, [neg_b, xa, xd])
         pick_payslips(7, 42)
-        d_last = absences(7)
+        pick_absences(7)
         join(6, both, [neg_b, xa, xd])
-        for h in range(2):
-            pick_half(xd, 7, h, d_last, l_pos3, ring.tile([P, HALF], F32, name="xd7%d" % h, tag="xd", bufs=6))
-            join(7, (h,), [neg_b, xa, xd])
+        join(7, both, [neg_b, xa, xd])
         quantise_z(1, 0)
         quantise_z(1, 1)
         second_stage(0)

@@ -19,9 +19,28 @@ ACT = mybir.ActivationFunctionType
 
 P = 128
 KIB = 1024
-NB = 512
+PASS = 512
+BANK = 512
+BLOCKS = 16
 HALF = J // 2
 SLICES = H // P
+PASS_SLICES = PASS // P
+WINDOWS = 10
+PICKED_D = 6
+PRODUCT_BANKS, JOIN_BANKS, TURN_BANKS = 4, 2, 2
+
+AREA_A = 0
+V3_GOT, V_W0 = AREA_A + 8, AREA_A + 12
+AREA_E = 16
+AREA_B = 24
+V3_WORDS = AREA_B + 4
+V3_ROWS = 44
+AREA_C = 48
+W1_11, W3_1 = AREA_C + 4, AREA_C + 12
+V2_W, W_PLANE, V2_PLANE, NEG_B0, V_W1, V3_W = 72, 76, 77, 78, 80, 84
+CAST = [88, 92, 96, 100]
+NEG_B4, W2_CODES, V_PLANE, V3_PLANE, V2_GOT, V_GOT = 104, 106, 108, 109, 110, 111
+PICKED_KIB = 2
 
 
 def tile_list_payslip_discrepancy_features_kernel(
@@ -36,61 +55,63 @@ def tile_list_payslip_discrepancy_features_kernel(
         arena = ctx.enter_context(tc.tile_pool(name="arena", bufs=1))
         psum = ctx.enter_context(tc.psum_pool(name="psum", bufs=1))
 
+        def placed(shape, dtype, name, kib):
+            return arena.tile(shape, dtype, name=name, align_bytes=64, offset=kib * KIB)
+
         def load_list(src, name):
             lst = keep.tile(list(src.shape), U16, name=name)
             nc.sync.dma_start(lst[:], src)
             return lst
 
-        def placed(shape, dtype, name, kib):
-            return arena.tile(shape, dtype, name=name, align_bytes=64, offset=kib * KIB)
-
-        def zeroed_plane(width, name, engine, kib):
+        def zeroed_plane(width, name, kib):
             plane = placed([P, width], U8, name, kib)
-            engine.memset(plane[:].bitcast(I32), 0)
+            nc.gpsimd.memset(plane[:].bitcast(I32), 0)
             return plane
 
-        def load_scale_rows(plane, src, quadrants):
+        def load_weight_scales(plane, src, quadrants, queue):
             passes = src.shape[0]
             for q in quadrants:
-                nc.sync.dma_start(
+                queue.dma_start(
                     out=plane[32 * q : 32 * q + 4 * passes, :].bitcast(I32),
                     in_=src[:, 4 * q : 4 * q + 4, :].bitcast(I32),
                 )
 
-        def scale_window(src, name, kib):
-            first = P - 16 * src.shape[0]
-            win = placed([P, T], U8, name, kib)
-            nc.vector.memset(win[0:first, :].bitcast(I32), 0)
-            nc.sync.dma_start(out=win[first:, :].bitcast(I32), in_=src.rearrange("a q t -> (a q) t").bitcast(I32))
-            return win
+        def load_table_scales(src, name, kib):
+            unused = P - BLOCKS * src.shape[0]
+            scale_rows = placed([P, T], U8, name, kib)
+            nc.vector.memset(scale_rows[0:unused, :].bitcast(I32), 0)
+            nc.sync.dma_start(
+                out=scale_rows[unused:, :].bitcast(I32), in_=src.rearrange("a q t -> (a q) t").bitcast(I32)
+            )
+            return scale_rows
 
-        def move_scale_rows(plane, got, passes, a, quadrants):
+        def move_picked_scales(plane, got, passes, a, quadrants, queue):
             for q in quadrants:
-                row = P - 16 * passes + 16 * a + 4 * q
-                nc.sync.dma_start(
+                row = P - BLOCKS * passes + BLOCKS * a + 4 * q
+                queue.dma_start(
                     out=plane[32 * q + 4 * a : 32 * q + 4 * a + 4, :].bitcast(I32),
                     in_=got[row : row + 4, :].bitcast(I32),
                 )
 
-        def load_table(words, a, name, kib):
-            win = placed([P, T], I32, name, kib)
-            nc.sync.dma_start(out=win[:], in_=words[a].rearrange("p t i -> p (t i)").bitcast(I32))
-            return win
+        def load_table_words(words, a, name, kib):
+            table = placed([P, T], I32, name, kib)
+            nc.sync.dma_start(out=table[:], in_=words[a].rearrange("p t i -> p (t i)").bitcast(I32))
+            return table
 
-        def pick_words(win, lst, name, kib):
+        def pick_words(table, lst, name, kib):
             got = placed([P, S], U32, name, kib)
-            nc.vector.tensor_copy(got[:], win[:].bitcast(U32).indirect(lst[:]))
+            nc.vector.tensor_copy(got[:], table[:].bitcast(U32).indirect(lst[:]))
             return got
 
-        def pick_scales(plane, lst, name, kib):
+        def pick_scales(scale_rows, lst, name, kib):
             got = placed([P, S], U8, name, kib)
-            nc.vector.tensor_copy(got[:], plane[:].indirect(lst[:]))
+            nc.vector.tensor_copy(got[:], scale_rows[:].indirect(lst[:]))
             return got
 
-        def load_weight(w, a, h, name, kib):
-            raw = placed([P, 4, NB], F32, name, kib)
-            rows = w[512 * a : 512 * (a + 1), NB * h : NB * (h + 1)]
-            nc.sync.dma_start(out=raw[:], in_=rows.rearrange("(p i) c -> p i c", i=4))
+        def load_weight(w, a, chunk, name, kib):
+            raw = placed([P, 4, BANK], F32, name, kib)
+            src = w[PASS * a : PASS * (a + 1), BANK * chunk : BANK * (chunk + 1)]
+            nc.sync.dma_start(out=raw[:], in_=src.rearrange("(p i) c -> p i c", i=4))
             return raw
 
         def quantise(grouped, name):
@@ -104,69 +125,72 @@ def tile_list_payslip_discrepancy_features_kernel(
             return codes, scales
 
         def quantise_weight(raw, name, kib):
-            grouped = placed([P, NB, 4], BF16, name + "_grouped", kib)
-            copy = nc.vector.tensor_copy if name in () else nc.scalar.copy
-            copy(
+            grouped = placed([P, BANK, 4], BF16, name + "_grouped", kib)
+            nc.scalar.copy(
                 out=grouped[:].rearrange("p (c n) (u e) -> p c u n e", n=4, e=2),
                 in_=raw[:].rearrange("p (u e) (c n) -> p c u n e", n=4, e=2),
             )
             return quantise(grouped, name)
 
-        def first_stage(stationary, moving, func, name, kib=None):
-            if kib is None:
-                win = ring.tile([P, S], F32, name=name, tag="win", bufs=10)
-            else:
-                win = placed([P, S], F32, name, kib)
-            for h in range(S // NB):
-                cols = slice(NB * h, NB * (h + 1))
-                acc = psum.tile([P, NB], F32, name="acc", tag="acc", bufs=4)
-                for a, ((lw, ls), (rw, rs)) in enumerate(zip(stationary, moving)):
+        def first_stage(stationary, moving, evacuate, window):
+            for part in range(S // BANK):
+                cols = slice(BANK * part, BANK * (part + 1))
+                acc = psum.tile([P, BANK], F32, name="acc", tag="product", bufs=PRODUCT_BANKS)
+                for a, ((w_codes, w_scales), (t_codes, t_scales)) in enumerate(zip(stationary, moving)):
                     nc.tensor.matmul_mx(
-                        out=acc[:], lhsT=lw, lhsT_scale=ls,
-                        rhs=rw[:, cols].bitcast(FP8X4), rhs_scale=rs[:, cols],
+                        out=acc[:], lhsT=w_codes, lhsT_scale=w_scales,
+                        rhs=t_codes[:, cols].bitcast(FP8X4), rhs_scale=t_scales[:, cols],
                         start=(a == 0), stop=(a == len(moving) - 1),
                     )
-                if func is None:
-                    nc.scalar.copy(out=win[:, cols], in_=acc[:])
-                else:
-                    nc.scalar.activation(out=win[:, cols], in_=acc[:], func=func)
-            return win
+                evacuate(window[:, cols], acc[:])
+            return window
+
+        def next_window(name):
+            return ring.tile([P, S], F32, name=name, tag="window", bufs=WINDOWS)
+
+        def gelu(dst, src):
+            nc.scalar.activation(out=dst, in_=src, func=ACT.Gelu_apprx_tanh)
+
+        def chunk_columns(quantised, s):
+            codes, scales = quantised
+            cols = slice(P * (s % PASS_SLICES), P * (s % PASS_SLICES + 1))
+            return codes[:, cols].bitcast(FP8X4), scales[:, cols]
 
         l_offs2 = load_list(offs2, "l_offs2")
-        v2_rows = scale_window(tab2_scales, "v2_rows", 24)
+        v2_rows = load_table_scales(tab2_scales, "v2_rows", AREA_B)
         l_offs = load_list(offs, "l_offs")
-        v_rows = scale_window(tab_scales, "v_rows", 48)
+        v_rows = load_table_scales(tab_scales, "v_rows", AREA_C)
         l_pos2 = load_list(pos2, "l_pos2")
         l_pos1 = load_list(pos1, "l_pos1")
         l_pos3 = load_list(pos3, "l_pos3")
-        v2_win = load_table(tab2_words, 0, "v2_win", 0)
+        v2_table = load_table_words(tab2_words, 0, "v2_table", AREA_A)
         l_offs3 = load_list(offs3, "l_offs3")
-        w2_plane = zeroed_plane(H, "w2_plane", nc.gpsimd, 76)
-        v2_s = zeroed_plane(S, "v2_s", nc.gpsimd, 77)
-        v3_rows = scale_window(tab3_scales, "v3_rows", 44)
-        w2_codes = placed([P, 2 * H], U8, "w2_codes", 106)
+        w2_plane = zeroed_plane(H, "w2_plane", W_PLANE)
+        v2_plane = zeroed_plane(S, "v2_plane", V2_PLANE)
+        v3_rows = load_table_scales(tab3_scales, "v3_rows", V3_ROWS)
+        load_weight_scales(w2_plane, w2_scales, range(3), nc.sync)
+        w1_00 = load_weight(w1, 0, 0, "w1_00", AREA_E)
+        w2_codes = placed([P, 2 * H], U8, "w2_codes", W2_CODES)
         nc.sync.dma_start(out=w2_codes[:].bitcast(I32), in_=w2_words[0].bitcast(I32))
-        load_scale_rows(w2_plane, w2_scales, range(3))
-        w1_00 = load_weight(w1, 0, 0, "w1_00", 16)
-        load_scale_rows(w2_plane, w2_scales, range(3, 4))
-        gains_rows = keep.tile([P, P], F32, name="gains_rows")
-        nc.gpsimd.memset(gains_rows[:], 0.0)
-        v_s = zeroed_plane(S, "v_s", nc.gpsimd, 108)
-        v3_s = zeroed_plane(S, "v3_s", nc.gpsimd, 109)
+        load_weight_scales(w2_plane, w2_scales, range(3, 4), nc.sync)
+        gain_rows = keep.tile([P, P], F32, name="gain_rows")
+        nc.gpsimd.memset(gain_rows[:], 0.0)
+        v_plane = zeroed_plane(S, "v_plane", V_PLANE)
+        v3_plane = zeroed_plane(S, "v3_plane", V3_PLANE)
         ident = keep.tile([P, P], F32, name="ident")
         make_identity(nc, ident[:])
 
-        v2_got = pick_scales(v2_rows, l_offs2, "v2_got", 110)
-        move_scale_rows(v2_s, v2_got, 1, 0, range(4))
-        v_win0 = load_table(tab_words, 0, "v_win0", 24)
-        nc.sync.dma_start(out=gains_rows[0:SLICES, :], in_=gb.rearrange("(s p) -> s p", p=P))
-        nc.sync.dma_start(out=gains_rows[SLICES : 2 * SLICES, :], in_=ga.rearrange("(s p) -> s p", p=P))
-        v_got = pick_scales(v_rows, l_offs, "v_got", 111)
+        v2_got = pick_scales(v2_rows, l_offs2, "v2_got", V2_GOT)
+        move_picked_scales(v2_plane, v2_got, 1, 0, range(4), nc.sync)
+        v_table0 = load_table_words(tab_words, 0, "v_table0", AREA_B)
+        nc.sync.dma_start(out=gain_rows[0:SLICES, :], in_=gb.rearrange("(s p) -> s p", p=P))
+        nc.sync.dma_start(out=gain_rows[SLICES : 2 * SLICES, :], in_=ga.rearrange("(s p) -> s p", p=P))
+        v_got = pick_scales(v_rows, l_offs, "v_got", V_GOT)
 
-        gains_t = psum.tile([P, P], F32, name="gains_t", tag="turn", bufs=2)
-        nc.tensor.transpose(gains_t[:], gains_rows[:], ident[:])
+        gain_cols = psum.tile([P, P], F32, name="gain_cols", tag="turn", bufs=TURN_BANKS)
+        nc.tensor.transpose(gain_cols[:], gain_rows[:], ident[:])
         gains = keep.tile([P, 2 * SLICES], F32, name="gains")
-        nc.scalar.copy(out=gains[:], in_=gains_t[:, 0 : 2 * SLICES])
+        nc.scalar.copy(out=gains[:], in_=gain_cols[:, 0 : 2 * SLICES])
 
         neg_b = {}
         xa = {}
@@ -174,166 +198,150 @@ def tile_list_payslip_discrepancy_features_kernel(
 
         def agreements(s):
             stationary = [(w2_codes[:, 2 * P * s : 2 * P * (s + 1)].bitcast(FP4X4), w2_plane[:, P * s : P * (s + 1)])]
-            return first_stage(stationary, [(v2_w, v2_s)], ACT.Gelu_apprx_tanh, "e%d" % s)
+            return first_stage(stationary, [(v2_w, v2_plane)], gelu, next_window("e%d" % s))
 
-        def payslips(s, kib=None):
-            h, c = divmod(s, 4)
-            cols = slice(P * c, P * (c + 1))
-            stationary = [(w1_q[a, h][0][:, cols].bitcast(FP8X4), w1_q[a, h][1][:, cols]) for a in range(2)]
-            moving = [(v_w[a], v_s[4 * a :, :]) for a in range(2)]
-            return first_stage(stationary, moving, None, "a%d" % s, kib)
+        def pick_agreements(s, window, kib):
+            neg_b[s] = placed([P, J], F32, "neg_b%d" % s, kib)
+            nc.vector.tensor_copy(neg_b[s][:], window[:].indirect(l_pos2[:]))
+            nc.vector.tensor_scalar(neg_b[s][:], neg_b[s][:], gains[:, s : s + 1], -1.0, ALU.mult, ALU.mult)
 
-        def absences(s):
-            h, c = divmod(s, 4)
-            cols = slice(P * c, P * (c + 1))
-            stationary = [(w3_q[h][0][:, cols].bitcast(FP8X4), w3_q[h][1][:, cols])]
-            return first_stage(stationary, [(v3_w, v3_s)], None, "d%d" % s)
-
-        def pick(into, s, win, lst, got):
-            nc.vector.tensor_copy(got[:], win[:].indirect(lst[:]))
-            for h in range(2):
-                into[s, h] = got[:, HALF * h : HALF * (h + 1)]
-
-        def pick_half(into, s, h, win, lst, got):
-            nc.vector.tensor_copy(got[:], win[:].indirect(lst[:, 16 * h : 16 * (h + 1)]))
-            into[s, h] = got[:]
-
-        def pick_agreements(s, win, kib):
-            got = placed([P, J], F32, "neg_b%d" % s, kib)
-            pick(neg_b, s, win, l_pos2, got)
-            nc.vector.tensor_scalar(got[:], got[:], gains[:, s : s + 1], -1.0, ALU.mult, ALU.mult)
-
-        def pick_payslips(s, kib, win_kib=None):
-            pick(xa, s, payslips(s, win_kib), l_pos1, placed([P, J], F32, "xa%d" % s, kib))
+        def pick_payslips(s, window):
+            stationary = [chunk_columns(w1_q[a, s // PASS_SLICES], s) for a in range(2)]
+            moving = [(v_w[a], v_plane[4 * a :, :]) for a in range(2)]
+            first_stage(stationary, moving, nc.scalar.copy, window)
+            xa[s] = placed([P, J], F32, "xa%d" % s, V3_WORDS + PICKED_KIB * s)
+            nc.vector.tensor_copy(xa[s][:], window[:].indirect(l_pos1[:]))
 
         def pick_absences(s):
-            pick(xd, s, absences(s), l_pos3, ring.tile([P, J], F32, name="xd%d" % s, tag="xd", bufs=6))
+            stationary = [chunk_columns(w3_q[s // PASS_SLICES], s)]
+            window = first_stage(stationary, [(v3_w, v3_plane)], nc.scalar.copy, next_window("d%d" % s))
+            xd[s] = ring.tile([P, J], F32, name="xd%d" % s, tag="xd", bufs=PICKED_D)
+            nc.vector.tensor_copy(xd[s][:], window[:].indirect(l_pos3[:]))
 
         z_rows = {
             (b, h): keep.tile([P, 2, 2, P, 2], BF16, name="z_rows%d%d" % (b, h)) for b in range(2) for h in range(2)
         }
         z_q = {}
 
-        def join(s, halves, terms, copy=nc.scalar.copy):
-            b, c = divmod(s, 4)
-            bank = psum.tile([P, len(halves), 2, P], F32, name="join%d" % s, tag="join", bufs=2)
-            steps = [(term, i, h, g) for term in terms for i, h in enumerate(halves) for g in range(2)]
-            for n, (term, i, h, g) in enumerate(steps):
+        def join(s):
+            b, c = divmod(s, PASS_SLICES)
+            terms = [xd[s], neg_b[s], xa[s]] if s < JOIN_BANKS else [neg_b[s], xa[s], xd[s]]
+            bank = psum.tile([P, 2, 2, P], F32, name="join%d" % s, tag="join", bufs=JOIN_BANKS)
+            steps = [(term, h, g) for term in terms for h in range(2) for g in range(2)]
+            for n, (term, h, g) in enumerate(steps):
+                j0 = HALF * h + P * g
                 nc.tensor.matmul(
-                    bank[:, i, g, :], lhsT=term[s, h][:, P * g : P * (g + 1)], rhs=ident[:], is_transpose=True,
+                    bank[:, h, g, :], lhsT=term[:, j0 : j0 + P], rhs=ident[:], is_transpose=True,
                     start=(n == 0), stop=(n == len(steps) - 1),
                 )
-            if (s, halves[0]) in ():
-                copy = nc.vector.tensor_copy
-            for i, h in enumerate(halves):
-                copy(
+            for h in range(2):
+                nc.scalar.copy(
                     out=z_rows[b, h][:, :, :, 32 * c : 32 * (c + 1), :],
-                    in_=bank[:, i].rearrange("j g (q u e) -> j g u q e", u=2, e=2),
+                    in_=bank[:, h].rearrange("j g (p u e) -> j g u p e", u=2, e=2),
                 )
 
         def quantise_z(b, h):
             words = z_rows[b, h][:].rearrange("j g u p e -> j (g u p e)").bitcast(F32)
             grouped = ring.tile([P, HALF, 4], BF16, name="z_grouped", tag="z_grouped", bufs=2, align_bytes=64)
-            bank = psum.tile([P, 4, P], F32, name="turn", tag="turn", bufs=2)
+            bank = psum.tile([P, 4, P], F32, name="turn", tag="turn", bufs=TURN_BANKS)
             for n in range(4):
                 nc.tensor.transpose(bank[:, n, :], words[:, P * n : P * (n + 1)], ident[:])
-            copy = nc.vector.tensor_copy if (b, h) in () else nc.scalar.copy
-            copy(
+            nc.scalar.copy(
                 out=grouped[:].rearrange("p j i -> p (j i)").bitcast(F32).rearrange("p (g j u) -> p g j u", g=2, u=2),
                 in_=bank[:].rearrange("p (g u) j -> p g j u", u=2),
             )
             z_q[b, h] = quantise(grouped, "z_%d%d" % (b, h))
 
         def second_stage(h):
+            half = slice(HALF * h, HALF * (h + 1))
             for pair in range(SLICES // 2):
-                acc = psum.tile([P, 2, HALF], F32, name="y", tag="acc", bufs=4)
+                y = psum.tile([P, 2, HALF], F32, name="y", tag="product", bufs=PRODUCT_BANKS)
                 for b in range(2):
+                    z_codes, z_scales = z_q[b, h]
                     for i in range(2):
                         cols = slice(P * (2 * pair + i), P * (2 * pair + i + 1))
                         nc.tensor.matmul_mx(
-                            out=acc[:, i, :], lhsT=w4_codes[:, b, cols].bitcast(FP8X4),
+                            out=y[:, i, :], lhsT=w4_codes[:, b, cols].bitcast(FP8X4),
                             lhsT_scale=w4_plane[4 * b :, cols],
-                            rhs=z_q[b, h][0][:].bitcast(FP8X4), rhs_scale=z_q[b, h][1][:],
+                            rhs=z_codes[:].bitcast(FP8X4), rhs_scale=z_scales[:],
                             start=(b, i) == (0, 0), stop=(b, i) == (1, 1),
                         )
-                res = ring.tile([P, 2, HALF], F32, name="res", tag="res", bufs=8)
+                res = ring.tile([P, 2, HALF], F32, name="res", tag="res", bufs=SLICES)
                 for i in range(2):
                     s = 2 * pair + i
                     nc.vector.scalar_tensor_tensor(
-                        out=res[:, i, :], in0=xa[s, h], scalar=gains[:, SLICES + s : SLICES + s + 1], in1=acc[:, i, :],
-                        op0=ALU.mult, op1=ALU.subtract,
+                        out=res[:, i, :], in0=xa[s][:, half], scalar=gains[:, SLICES + s : SLICES + s + 1],
+                        in1=y[:, i, :], op0=ALU.mult, op1=ALU.subtract,
                     )
-                nc.scalar.activation(out=res[:], in_=res[:], func=ACT.Abs)
-                rows = out[2 * P * pair : 2 * P * (pair + 1), HALF * h : HALF * (h + 1)]
-                nc.sync.dma_start(out=rows.rearrange("(i p) j -> p i j", i=2), in_=res[:])
+                dst = out[2 * P * pair : 2 * P * (pair + 1), half].rearrange("(i p) j -> p i j", i=2)
+                last = h == 1 and pair == SLICES // 2 - 1
+                for share in [slice(0, 1), slice(1, 2)] if last else [slice(0, 2)]:
+                    nc.scalar.activation(out=res[:, share, :], in_=res[:, share, :], func=ACT.Abs)
+                    nc.sync.dma_start(out=dst[:, share, :], in_=res[:, share, :])
 
         w1_q = {}
-        v2_w = placed([P, S], U32, "v2_w", 72)
-        for h in range(2):
-            nc.vector.tensor_copy(
-                v2_w[:, NB * h : NB * (h + 1)], v2_win[:].bitcast(U32).indirect(l_offs2[:, 32 * h : 32 * (h + 1)])
-            )
-        w1_10 = load_weight(w1, 1, 0, "w1_10", 0)
-        v_win1 = load_table(tab_words, 1, "v_win1", 48)
-        v3_got = pick_scales(v3_rows, l_offs3, "v3_got", 8)
-        move_scale_rows(v_s, v_got, 2, 0, range(3))
-        w1_q[0, 0] = quantise_weight(w1_00, "w1q_00", 88)
-        w3_0 = load_weight(w3, 0, 0, "w3_0", 16)
-        move_scale_rows(v_s, v_got, 2, 0, range(3, 4))
-        move_scale_rows(v_s, v_got, 2, 1, range(4))
-        pick_agreements(0, agreements(0), 78)
-        v_w = [pick_words(v_win0, l_offs, "v_w0", 12)]
-        v3_win = load_table(tab3_words, 0, "v3_win", 28)
-        move_scale_rows(v3_s, v3_got, 1, 0, range(4))
-        pick_agreements(1, agreements(1), 24)
-        pick_agreements(2, agreements(2), 26)
-        w1_q[1, 0] = quantise_weight(w1_10, "w1q_10", 92)
-        w1_01 = load_weight(w1, 0, 1, "w1_01", 0)
-        v_w.append(pick_words(v_win1, l_offs, "v_w1", 80))
-        w1_11 = load_weight(w1, 1, 1, "w1_11", 52)
-        w3_1 = load_weight(w3, 0, 1, "w3_1", 60)
-        pick_agreements(3, agreements(3), 48)
-        pick_agreements(4, agreements(4), 104)
+        v2_w = placed([P, S], U32, "v2_w", V2_W)
+        for part in range(S // BANK):
+            entries = l_offs2[:, BANK // 16 * part : BANK // 16 * (part + 1)]
+            nc.vector.tensor_copy(v2_w[:, BANK * part : BANK * (part + 1)], v2_table[:].bitcast(U32).indirect(entries))
+        w1_10 = load_weight(w1, 1, 0, "w1_10", AREA_A)
+        v_table1 = load_table_words(tab_words, 1, "v_table1", AREA_C)
+        v3_got = pick_scales(v3_rows, l_offs3, "v3_got", V3_GOT)
+        move_picked_scales(v_plane, v_got, 2, 0, range(3), nc.sync)
+        w1_q[0, 0] = quantise_weight(w1_00, "w1q_00", CAST[0])
+        w3_0 = load_weight(w3, 0, 0, "w3_0", AREA_E)
+        move_picked_scales(v_plane, v_got, 2, 0, range(3, 4), nc.sync)
+        move_picked_scales(v_plane, v_got, 2, 1, range(4), nc.sync)
+        pick_agreements(0, agreements(0), NEG_B0)
+        v_w = [pick_words(v_table0, l_offs, "v_w0", V_W0)]
+        v3_table = load_table_words(tab3_words, 0, "v3_table", V3_WORDS)
+        move_picked_scales(v3_plane, v3_got, 1, 0, range(4), nc.gpsimd)
+        pick_agreements(1, agreements(1), AREA_B)
+        pick_agreements(2, agreements(2), AREA_B + PICKED_KIB)
+        w1_q[1, 0] = quantise_weight(w1_10, "w1q_10", CAST[1])
+        w1_01 = load_weight(w1, 0, 1, "w1_01", AREA_A)
+        v_w.append(pick_words(v_table1, l_offs, "v_w1", V_W1))
+        w1_11 = load_weight(w1, 1, 1, "w1_11", W1_11)
+        w3_1 = load_weight(w3, 0, 1, "w3_1", W3_1)
+        pick_agreements(3, agreements(3), AREA_C)
+        pick_agreements(4, agreements(4), NEG_B4)
         late = {s: agreements(s) for s in range(5, SLICES)}
-        w4_plane = zeroed_plane(H, "w4_plane", nc.gpsimd, 76)
-        load_scale_rows(w4_plane, w4_scales, range(4))
-        w3_q = [quantise_weight(w3_0, "w3q_0", 88)]
-        v3_w = pick_words(v3_win, l_offs3, "v3_w", 84)
-        both = (0, 1)
-        pick_payslips(0, 28, 16)
-        pick_payslips(1, 30)
-        pick_payslips(2, 32)
-        w1_q[0, 1] = quantise_weight(w1_01, "w1q_01", 92)
-        w4_codes = placed([P, 2, H], I32, "w4_codes", 0)
+        w4_plane = zeroed_plane(H, "w4_plane", W_PLANE)
+        load_weight_scales(w4_plane, w4_scales, range(4), nc.gpsimd)
+        w3_q = [quantise_weight(w3_0, "w3q_0", CAST[0])]
+        v3_w = pick_words(v3_table, l_offs3, "v3_w", V3_W)
+
+        pick_payslips(0, placed([P, S], F32, "a0", AREA_E))
+        pick_payslips(1, next_window("a1"))
+        pick_payslips(2, next_window("a2"))
+        w1_q[0, 1] = quantise_weight(w1_01, "w1q_01", CAST[1])
+        w4_codes = placed([P, 2, H], I32, "w4_codes", AREA_A)
         nc.sync.dma_start(out=w4_codes[:], in_=w4_words.rearrange("a p c i -> p a (c i)").bitcast(I32))
-        pick_agreements(5, late[5], 92)
+        pick_agreements(5, late[5], CAST[1])
         pick_absences(0)
         pick_absences(1)
-        pick_payslips(3, 34)
-        w1_q[1, 1] = quantise_weight(w1_11, "w1q_11", 96)
-        pick_agreements(6, late[6], 96)
+        pick_payslips(3, next_window("a3"))
+        w1_q[1, 1] = quantise_weight(w1_11, "w1q_11", CAST[2])
+        pick_agreements(6, late[6], CAST[2])
         pick_absences(2)
-        join(0, both, [xd, neg_b, xa])
+        join(0)
         pick_absences(3)
-        join(1, both, [xd, neg_b, xa])
-        w3_q.append(quantise_weight(w3_1, "w3q_1", 100))
-        pick_agreements(7, late[7], 100)
-        pick_payslips(4, 36)
-        join(2, both, [neg_b, xa, xd])
+        join(1)
+        w3_q.append(quantise_weight(w3_1, "w3q_1", CAST[3]))
+        pick_agreements(7, late[7], CAST[3])
+
+        pick_payslips(4, next_window("a4"))
+        join(2)
         pick_absences(4)
-        join(3, both, [neg_b, xa, xd])
-        pick_payslips(5, 38)
-        pick_absences(5)
-        quantise_z(0, 0)
-        quantise_z(0, 1)
-        join(4, both, [neg_b, xa, xd])
-        pick_payslips(6, 40)
-        pick_absences(6)
-        join(5, both, [neg_b, xa, xd])
-        pick_payslips(7, 42)
-        pick_absences(7)
-        join(6, both, [neg_b, xa, xd])
-        join(7, both, [neg_b, xa, xd])
+        join(3)
+        for s in range(5, SLICES):
+            pick_payslips(s, next_window("a%d" % s))
+            pick_absences(s)
+            if s - 1 == PASS_SLICES:
+                quantise_z(0, 0)
+                quantise_z(0, 1)
+            join(s - 1)
+        join(SLICES - 1)
         quantise_z(1, 0)
         quantise_z(1, 1)
         second_stage(0)

from contextlib import ExitStack

import concourse.mybir as mybir
from concourse.masks import make_identity

K, K2, H, T, S, J = 1024, 512, 1024, 4096, 1024, 512
FLOPS = 2 * (K * H * S + 2 * K2 * H * S + H * H * J)

F32 = mybir.dt.float32
BF16 = mybir.dt.bfloat16
I32 = mybir.dt.int32
U32 = mybir.dt.uint32
U16 = mybir.dt.uint16
U8 = mybir.dt.uint8
FP8X4 = mybir.dt.float8_e4m3fn_x4
FP4X4 = mybir.dt.float4_e2m1fn_x4
ALU = mybir.AluOpType
ACT = mybir.ActivationFunctionType

P = 128
KIB = 1024
PASS = 512
BANK = 512
BLOCKS = 16
HALF = J // 2
SLICES = H // P
PASS_SLICES = PASS // P
WINDOWS = 10
PICKED_D = 6
PRODUCT_BANKS, JOIN_BANKS, TURN_BANKS = 4, 2, 2

AREA_A = 0
V3_GOT, V_W0 = AREA_A + 8, AREA_A + 12
AREA_E = 16
AREA_B = 24
V3_WORDS = AREA_B + 4
V3_ROWS = 44
AREA_C = 48
W1_11, W3_1 = AREA_C + 4, AREA_C + 12
V2_W, W_PLANE, V2_PLANE, NEG_B0, V_W1, V3_W = 72, 76, 77, 78, 80, 84
CAST = [88, 92, 96, 100]
NEG_B4, W2_CODES, V_PLANE, V3_PLANE, V2_GOT, V_GOT = 104, 106, 108, 109, 110, 111
PICKED_KIB = 2


def tile_list_payslip_discrepancy_features_kernel(
    tc, tab_words, tab_scales, tab2_words, tab2_scales, tab3_words, tab3_scales,
    offs, offs2, offs3, pos1, pos2, pos3, w1, w2_words, w2_scales, w3,
    w4_words, w4_scales, gb, ga, out,
):
    nc = tc.nc
    with ExitStack() as ctx:
        keep = ctx.enter_context(tc.tile_pool(name="keep", bufs=1))
        ring = ctx.enter_context(tc.tile_pool(name="ring", bufs=1))
        arena = ctx.enter_context(tc.tile_pool(name="arena", bufs=1))
        psum = ctx.enter_context(tc.psum_pool(name="psum", bufs=1))

        def placed(shape, dtype, name, kib):
            return arena.tile(shape, dtype, name=name, align_bytes=64, offset=kib * KIB)

        def load_list(src, name):
            lst = keep.tile(list(src.shape), U16, name=name)
            nc.sync.dma_start(lst[:], src)
            return lst

        def zeroed_plane(width, name, kib):
            plane = placed([P, width], U8, name, kib)
            nc.gpsimd.memset(plane[:].bitcast(I32), 0)
            return plane

        def load_weight_scales(plane, src, quadrants, queue):
            passes = src.shape[0]
            for q in quadrants:
                queue.dma_start(
                    out=plane[32 * q : 32 * q + 4 * passes, :].bitcast(I32),
                    in_=src[:, 4 * q : 4 * q + 4, :].bitcast(I32),
                )

        def load_table_scales(src, name, kib):
            unused = P - BLOCKS * src.shape[0]
            scale_rows = placed([P, T], U8, name, kib)
            nc.vector.memset(scale_rows[0:unused, :].bitcast(I32), 0)
            nc.sync.dma_start(
                out=scale_rows[unused:, :].bitcast(I32), in_=src.rearrange("a q t -> (a q) t").bitcast(I32)
            )
            return scale_rows

        def move_picked_scales(plane, got, passes, a, quadrants, queue):
            for q in quadrants:
                row = P - BLOCKS * passes + BLOCKS * a + 4 * q
                queue.dma_start(
                    out=plane[32 * q + 4 * a : 32 * q + 4 * a + 4, :].bitcast(I32),
                    in_=got[row : row + 4, :].bitcast(I32),
                )

        def load_table_words(words, a, name, kib):
            table = placed([P, T], I32, name, kib)
            nc.sync.dma_start(out=table[:], in_=words[a].rearrange("p t i -> p (t i)").bitcast(I32))
            return table

        def pick_words(table, lst, name, kib):
            got = placed([P, S], U32, name, kib)
            nc.vector.tensor_copy(got[:], table[:].bitcast(U32).indirect(lst[:]))
            return got

        def pick_scales(scale_rows, lst, name, kib):
            got = placed([P, S], U8, name, kib)
            nc.vector.tensor_copy(got[:], scale_rows[:].indirect(lst[:]))
            return got

        def load_weight(w, a, chunk, name, kib):
            raw = placed([P, 4, BANK], F32, name, kib)
            src = w[PASS * a : PASS * (a + 1), BANK * chunk : BANK * (chunk + 1)]
            nc.sync.dma_start(out=raw[:], in_=src.rearrange("(p i) c -> p i c", i=4))
            return raw

        def quantise(grouped, name):
            width = grouped.shape[1]
            codes = keep.tile([P, width], U32, name=name + "_codes", align_bytes=64)
            scales = keep.tile([P, width], U8, name=name + "_scales", align_bytes=64)
            nc.vector.quantize_mx(
                out=codes[:].bitcast(FP8X4), scales=scales[:],
                in_=grouped[:].rearrange("p c i -> p (c i)"),
            )
            return codes, scales

        def quantise_weight(raw, name, kib):
            grouped = placed([P, BANK, 4], BF16, name + "_grouped", kib)
            nc.scalar.copy(
                out=grouped[:].rearrange("p (c n) (u e) -> p c u n e", n=4, e=2),
                in_=raw[:].rearrange("p (u e) (c n) -> p c u n e", n=4, e=2),
            )
            return quantise(grouped, name)

        def first_stage(stationary, moving, evacuate, window):
            for part in range(S // BANK):
                cols = slice(BANK * part, BANK * (part + 1))
                acc = psum.tile([P, BANK], F32, name="acc", tag="product", bufs=PRODUCT_BANKS)
                for a, ((w_codes, w_scales), (t_codes, t_scales)) in enumerate(zip(stationary, moving)):
                    nc.tensor.matmul_mx(
                        out=acc[:], lhsT=w_codes, lhsT_scale=w_scales,
                        rhs=t_codes[:, cols].bitcast(FP8X4), rhs_scale=t_scales[:, cols],
                        start=(a == 0), stop=(a == len(moving) - 1),
                    )
                evacuate(window[:, cols], acc[:])
            return window

        def next_window(name):
            return ring.tile([P, S], F32, name=name, tag="window", bufs=WINDOWS)

        def gelu(dst, src):
            nc.scalar.activation(out=dst, in_=src, func=ACT.Gelu_apprx_tanh)

        def chunk_columns(quantised, s):
            codes, scales = quantised
            cols = slice(P * (s % PASS_SLICES), P * (s % PASS_SLICES + 1))
            return codes[:, cols].bitcast(FP8X4), scales[:, cols]

        l_offs2 = load_list(offs2, "l_offs2")
        v2_rows = load_table_scales(tab2_scales, "v2_rows", AREA_B)
        l_offs = load_list(offs, "l_offs")
        v_rows = load_table_scales(tab_scales, "v_rows", AREA_C)
        l_pos2 = load_list(pos2, "l_pos2")
        l_pos1 = load_list(pos1, "l_pos1")
        l_pos3 = load_list(pos3, "l_pos3")
        v2_table = load_table_words(tab2_words, 0, "v2_table", AREA_A)
        l_offs3 = load_list(offs3, "l_offs3")
        w2_plane = zeroed_plane(H, "w2_plane", W_PLANE)
        v2_plane = zeroed_plane(S, "v2_plane", V2_PLANE)
        v3_rows = load_table_scales(tab3_scales, "v3_rows", V3_ROWS)
        load_weight_scales(w2_plane, w2_scales, range(3), nc.sync)
        w1_00 = load_weight(w1, 0, 0, "w1_00", AREA_E)
        w2_codes = placed([P, 2 * H], U8, "w2_codes", W2_CODES)
        nc.sync.dma_start(out=w2_codes[:].bitcast(I32), in_=w2_words[0].bitcast(I32))
        load_weight_scales(w2_plane, w2_scales, range(3, 4), nc.sync)
        gain_rows = keep.tile([P, P], F32, name="gain_rows")
        nc.gpsimd.memset(gain_rows[:], 0.0)
        v_plane = zeroed_plane(S, "v_plane", V_PLANE)
        v3_plane = zeroed_plane(S, "v3_plane", V3_PLANE)
        ident = keep.tile([P, P], F32, name="ident")
        make_identity(nc, ident[:])

        v2_got = pick_scales(v2_rows, l_offs2, "v2_got", V2_GOT)
        move_picked_scales(v2_plane, v2_got, 1, 0, range(4), nc.sync)
        v_table0 = load_table_words(tab_words, 0, "v_table0", AREA_B)
        nc.sync.dma_start(out=gain_rows[0:SLICES, :], in_=gb.rearrange("(s p) -> s p", p=P))
        nc.sync.dma_start(out=gain_rows[SLICES : 2 * SLICES, :], in_=ga.rearrange("(s p) -> s p", p=P))
        v_got = pick_scales(v_rows, l_offs, "v_got", V_GOT)

        gain_cols = psum.tile([P, P], F32, name="gain_cols", tag="turn", bufs=TURN_BANKS)
        nc.tensor.transpose(gain_cols[:], gain_rows[:], ident[:])
        gains = keep.tile([P, 2 * SLICES], F32, name="gains")
        nc.scalar.copy(out=gains[:], in_=gain_cols[:, 0 : 2 * SLICES])

        neg_b = {}
        xa = {}
        xd = {}

        def agreements(s):
            stationary = [(w2_codes[:, 2 * P * s : 2 * P * (s + 1)].bitcast(FP4X4), w2_plane[:, P * s : P * (s + 1)])]
            return first_stage(stationary, [(v2_w, v2_plane)], gelu, next_window("e%d" % s))

        def pick_agreements(s, window, kib):
            neg_b[s] = placed([P, J], F32, "neg_b%d" % s, kib)
            nc.vector.tensor_copy(neg_b[s][:], window[:].indirect(l_pos2[:]))
            nc.vector.tensor_scalar(neg_b[s][:], neg_b[s][:], gains[:, s : s + 1], -1.0, ALU.mult, ALU.mult)

        def pick_payslips(s, window):
            stationary = [chunk_columns(w1_q[a, s // PASS_SLICES], s) for a in range(2)]
            moving = [(v_w[a], v_plane[4 * a :, :]) for a in range(2)]
            first_stage(stationary, moving, nc.scalar.copy, window)
            xa[s] = placed([P, J], F32, "xa%d" % s, V3_WORDS + PICKED_KIB * s)
            nc.vector.tensor_copy(xa[s][:], window[:].indirect(l_pos1[:]))

        def pick_absences(s):
            stationary = [chunk_columns(w3_q[s // PASS_SLICES], s)]
            window = first_stage(stationary, [(v3_w, v3_plane)], nc.scalar.copy, next_window("d%d" % s))
            xd[s] = ring.tile([P, J], F32, name="xd%d" % s, tag="xd", bufs=PICKED_D)
            nc.vector.tensor_copy(xd[s][:], window[:].indirect(l_pos3[:]))

        z_rows = {
            (b, h): keep.tile([P, 2, 2, P, 2], BF16, name="z_rows%d%d" % (b, h)) for b in range(2) for h in range(2)
        }
        z_q = {}

        def join(s):
            b, c = divmod(s, PASS_SLICES)
            terms = [xd[s], neg_b[s], xa[s]] if s < JOIN_BANKS else [neg_b[s], xa[s], xd[s]]
            bank = psum.tile([P, 2, 2, P], F32, name="join%d" % s, tag="join", bufs=JOIN_BANKS)
            steps = [(term, h, g) for term in terms for h in range(2) for g in range(2)]
            for n, (term, h, g) in enumerate(steps):
                j0 = HALF * h + P * g
                nc.tensor.matmul(
                    bank[:, h, g, :], lhsT=term[:, j0 : j0 + P], rhs=ident[:], is_transpose=True,
                    start=(n == 0), stop=(n == len(steps) - 1),
                )
            for h in range(2):
                nc.scalar.copy(
                    out=z_rows[b, h][:, :, :, 32 * c : 32 * (c + 1), :],
                    in_=bank[:, h].rearrange("j g (p u e) -> j g u p e", u=2, e=2),
                )

        def quantise_z(b, h):
            words = z_rows[b, h][:].rearrange("j g u p e -> j (g u p e)").bitcast(F32)
            grouped = ring.tile([P, HALF, 4], BF16, name="z_grouped", tag="z_grouped", bufs=2, align_bytes=64)
            bank = psum.tile([P, 4, P], F32, name="turn", tag="turn", bufs=TURN_BANKS)
            for n in range(4):
                nc.tensor.transpose(bank[:, n, :], words[:, P * n : P * (n + 1)], ident[:])
            nc.scalar.copy(
                out=grouped[:].rearrange("p j i -> p (j i)").bitcast(F32).rearrange("p (g j u) -> p g j u", g=2, u=2),
                in_=bank[:].rearrange("p (g u) j -> p g j u", u=2),
            )
            z_q[b, h] = quantise(grouped, "z_%d%d" % (b, h))

        def second_stage(h):
            half = slice(HALF * h, HALF * (h + 1))
            for pair in range(SLICES // 2):
                y = psum.tile([P, 2, HALF], F32, name="y", tag="product", bufs=PRODUCT_BANKS)
                for b in range(2):
                    z_codes, z_scales = z_q[b, h]
                    for i in range(2):
                        cols = slice(P * (2 * pair + i), P * (2 * pair + i + 1))
                        nc.tensor.matmul_mx(
                            out=y[:, i, :], lhsT=w4_codes[:, b, cols].bitcast(FP8X4),
                            lhsT_scale=w4_plane[4 * b :, cols],
                            rhs=z_codes[:].bitcast(FP8X4), rhs_scale=z_scales[:],
                            start=(b, i) == (0, 0), stop=(b, i) == (1, 1),
                        )
                res = ring.tile([P, 2, HALF], F32, name="res", tag="res", bufs=SLICES)
                for i in range(2):
                    s = 2 * pair + i
                    nc.vector.scalar_tensor_tensor(
                        out=res[:, i, :], in0=xa[s][:, half], scalar=gains[:, SLICES + s : SLICES + s + 1],
                        in1=y[:, i, :], op0=ALU.mult, op1=ALU.subtract,
                    )
                dst = out[2 * P * pair : 2 * P * (pair + 1), half].rearrange("(i p) j -> p i j", i=2)
                last = h == 1 and pair == SLICES // 2 - 1
                for share in [slice(0, 1), slice(1, 2)] if last else [slice(0, 2)]:
                    nc.scalar.activation(out=res[:, share, :], in_=res[:, share, :], func=ACT.Abs)
                    nc.sync.dma_start(out=dst[:, share, :], in_=res[:, share, :])

        w1_q = {}
        v2_w = placed([P, S], U32, "v2_w", V2_W)
        for part in range(S // BANK):
            entries = l_offs2[:, BANK // 16 * part : BANK // 16 * (part + 1)]
            nc.vector.tensor_copy(v2_w[:, BANK * part : BANK * (part + 1)], v2_table[:].bitcast(U32).indirect(entries))
        w1_10 = load_weight(w1, 1, 0, "w1_10", AREA_A)
        v_table1 = load_table_words(tab_words, 1, "v_table1", AREA_C)
        v3_got = pick_scales(v3_rows, l_offs3, "v3_got", V3_GOT)
        move_picked_scales(v_plane, v_got, 2, 0, range(3), nc.sync)
        w1_q[0, 0] = quantise_weight(w1_00, "w1q_00", CAST[0])
        w3_0 = load_weight(w3, 0, 0, "w3_0", AREA_E)
        move_picked_scales(v_plane, v_got, 2, 0, range(3, 4), nc.sync)
        move_picked_scales(v_plane, v_got, 2, 1, range(4), nc.sync)
        pick_agreements(0, agreements(0), NEG_B0)
        v_w = [pick_words(v_table0, l_offs, "v_w0", V_W0)]
        v3_table = load_table_words(tab3_words, 0, "v3_table", V3_WORDS)
        move_picked_scales(v3_plane, v3_got, 1, 0, range(4), nc.gpsimd)
        pick_agreements(1, agreements(1), AREA_B)
        pick_agreements(2, agreements(2), AREA_B + PICKED_KIB)
        w1_q[1, 0] = quantise_weight(w1_10, "w1q_10", CAST[1])
        w1_01 = load_weight(w1, 0, 1, "w1_01", AREA_A)
        v_w.append(pick_words(v_table1, l_offs, "v_w1", V_W1))
        w1_11 = load_weight(w1, 1, 1, "w1_11", W1_11)
        w3_1 = load_weight(w3, 0, 1, "w3_1", W3_1)
        pick_agreements(3, agreements(3), AREA_C)
        pick_agreements(4, agreements(4), NEG_B4)
        late = {s: agreements(s) for s in range(5, SLICES)}
        w4_plane = zeroed_plane(H, "w4_plane", W_PLANE)
        load_weight_scales(w4_plane, w4_scales, range(4), nc.gpsimd)
        w3_q = [quantise_weight(w3_0, "w3q_0", CAST[0])]
        v3_w = pick_words(v3_table, l_offs3, "v3_w", V3_W)

        pick_payslips(0, placed([P, S], F32, "a0", AREA_E))
        pick_payslips(1, next_window("a1"))
        pick_payslips(2, next_window("a2"))
        w1_q[0, 1] = quantise_weight(w1_01, "w1q_01", CAST[1])
        w4_codes = placed([P, 2, H], I32, "w4_codes", AREA_A)
        nc.sync.dma_start(out=w4_codes[:], in_=w4_words.rearrange("a p c i -> p a (c i)").bitcast(I32))
        pick_agreements(5, late[5], CAST[1])
        pick_absences(0)
        pick_absences(1)
        pick_payslips(3, next_window("a3"))
        w1_q[1, 1] = quantise_weight(w1_11, "w1q_11", CAST[2])
        pick_agreements(6, late[6], CAST[2])
        pick_absences(2)
        join(0)
        pick_absences(3)
        join(1)
        w3_q.append(quantise_weight(w3_1, "w3q_1", CAST[3]))
        pick_agreements(7, late[7], CAST[3])

        pick_payslips(4, next_window("a4"))
        join(2)
        pick_absences(4)
        join(3)
        for s in range(5, SLICES):
            pick_payslips(s, next_window("a%d" % s))
            pick_absences(s)
            if s - 1 == PASS_SLICES:
                quantise_z(0, 0)
                quantise_z(0, 1)
            join(s - 1)
        join(SLICES - 1)
        quantise_z(1, 0)
        quantise_z(1, 1)
        second_stage(0)
        second_stage(1)
